import numpy as np, ml_dtypes
CORES = [1,5,17,21,33,37,49,53]
N = 8
BF = ml_dtypes.bfloat16
def gentries(a):
    return np.ascontiguousarray(a.reshape(8, 16, -1).transpose(0, 2, 1)).reshape(8, -1)
def gtable(e):
    e = np.asarray(e); return np.ascontiguousarray(e.reshape(8, -1, 16).transpose(0, 2, 1)).reshape(128, -1).astype(np.int32)
WX, WV, C, K, RO, TH = 4096, 4096, 384, 8, 5, 12
def flip(P, m):
    k = np.arange(K); m = np.asarray(m)[..., None]
    return np.take_along_axis(P, np.where(k <= m, m - k, k), -1)
def place(u):
    return (((u * u) >> 5) + 37 * u) & (WV - 1)
def slots(F, w):
    u = np.add.reduce(F * w[:, :, None], axis=1) & 4095
    return u, place(u)
def prints(X, Q):
    n, c = Q.shape[:2]; a = np.take_along_axis(X, Q.reshape(n, 1, c * K), 2).reshape(n, 16, c, K)
    return np.add.reduce(a * np.arange(K), axis=3) & 255
def parts(rng):
    X = rng.integers(0, 256, (N, 8, 16, WX)); w = rng.integers(0, 16, (N, 8, 16)); R = C >> 3; P = []; S = []; gg = np.arange(8)[:, None]
    a = rng.integers(0, WX, (8, R, K)); ma = rng.integers(1, K, (8, R))
    for q in range(N):
        roots = np.concatenate([a, rng.integers(0, WX, (8, R, K))], axis=1); ms = np.concatenate([ma, rng.integers(1, K, (8, R))], axis=1)
        fam = rng.integers(0, 2 * R, (8, C)); root = roots[gg, fam]; m = ms[gg, fam]
        kind = rng.integers(0, 4, (8, C)); m1 = rng.integers(1, K, (8, C)); m2 = rng.integers(0, K, (8, C))
        one = np.where(kind == 1, 0, np.where(kind == 2, m, m1))
        P.append(flip(flip(root, one), np.where(kind == 3, m2, 0)))
        S.append(np.where(kind == 0, m1, np.where(kind == 3, rng.integers(0, K, (8, C)), m)))
    return X, w, np.stack(P), np.stack(S)
def junk(rng, share):
    return np.where(rng.random((N, 8, 1, WV)) < share, rng.integers(0, 256, (N, 8, 16, WV)), 512)
def near(rng, F, tol, n):
    o = np.argsort(rng.random(F.shape), axis=1)
    d = np.where(o < n, np.where(rng.random(F.shape) < 0.5, tol, np.minimum(rng.integers(0, 6, F.shape), tol)), tol + 1 + rng.choice(np.array([0, 0, 1, 40]), F.shape))
    z = np.where(rng.random(F.shape) < 0.5, F + d, F - d)
    return np.where(z < 0, F + d, np.where(z > 255, F - d, z))
def sow(rng, X, V, w, P, s):
    E = 6
    for q in range(N):
        for t in range(RO):
            r = (q - t) % N; c = rng.permutation(C)[:C >> 2]; n = len(c)
            st = P[r][:, c]; m = np.maximum(s[r][:, c], 1)
            if t & 1: st = flip(st, m)
            F = prints(X[q], flip(st, m)); h = slots(F, w[q])[1]
            np.put_along_axis(V[q], h[:, None, :], near(rng, F, rng.integers(2, 6, (8, 1, n)), rng.choice(np.array([11, 12, 12, 13, 16]), (8, 1, n))), 2)
            Q = flip(np.broadcast_to(st[:, :E, None], (8, E, K - 1, K)), np.broadcast_to(np.arange(1, K), (8, E, K - 1))).reshape(8, E * (K - 1), K)
            F = prints(X[q], Q); h = slots(F, w[q])[1]; e = (E >> 1) * (K - 1)
            z = near(rng, F, 2, rng.choice(np.array([12, 13, 16]), (8, 1, E * (K - 1)))); z[:, :, :e] = F[:, :, :e]
            np.put_along_axis(V[q], h[:, None, :], z, 2)
    return V
def pack(X, V, P, s, w):
    return {"x": np.ascontiguousarray(X.reshape(N, 128, WX)).astype(np.float32).astype(BF), "v": np.ascontiguousarray(V.reshape(N, 128, WV)).astype(np.float32).astype(BF),
            "lanes": np.stack([gtable(a.reshape(8, C * K)) for a in P]), "s0": np.ascontiguousarray(s).astype(np.int32), "wt": np.ascontiguousarray(w.reshape(N, 128, 1)).astype(np.int32)}
def setup_inputs(rng):
    X, w, P, s = parts(rng)
    return pack(X, sow(rng, X, junk(rng, 0.2), w, P, s), P, s, w)
def setup_inputs_spread(rng):
    X, w, P, s = parts(rng)
    X = (np.exp2(8 * rng.random((N, 8, 1, WX))) * rng.random((N, 8, 16, WX))).astype(np.int64)
    w = (16 * rng.random((N, 8, 16)) ** 3).astype(np.int64); w[:, :, 5] = 1 + 2 * rng.integers(0, 8, (N, 8))
    tb = (WX * rng.random((8, WX)) ** 3).astype(np.int64); tb[:, 0] = WX - 1
    P = np.stack([tb[g][P[:, g]] for g in range(8)], axis=1)
    s = np.where(rng.random(s.shape) < 0.3, (K * rng.random(s.shape) ** 3).astype(np.int64), s)
    return pack(X, sow(rng, X, junk(rng, 0.5), w, P, s), P, s, w)
def setup_inputs_ends(rng):
    X = 255 * rng.integers(0, 2, (N, 8, 16, WX)); w = 15 * rng.integers(0, 2, (N, 8, 16))
    V = np.where(rng.random((N, 8, 1, WV)) < 0.25, 512 * rng.integers(0, 2, (N, 8, 16, WV)), 512 * rng.integers(0, 2, (N, 8, 1, WV)))
    for g in range(8):
        kind = 3 - (g & 3); o = rng.permutation(16)
        X[:, g, :, 0] = 255 if kind == 1 else 0; X[:, g, :, WX - 1] = 255 if kind == 0 else 0
        if kind == 0: w[:, g] = 15
        if kind == 1: w[:, g, o[0]] = 15; w[:, g, o[1]] = 0
        if kind == 2:
            for i in o[:4]: X[:, g, i, WX - 1] = 255; w[:, g, i] = 15
        if kind == 3:
            for i in o[:3]: X[:, g, i, 0] = 255; w[:, g, i] = 15
    P = np.where(rng.random((N, 8, C, K)) < rng.random((N, 8, C, 1)), WX - 1, 0); s = (K - 1) * rng.integers(0, 2, (N, 8, C))
    for c in (0, 1, C - 2, C - 1): P[:, :, c] = 0
    for c in (2, C - 3): P[:, :, c] = WX - 1
    for c in (3, C - 4): P[:, :, c] = 0; P[:, :, c, 0] = WX - 1; s[:, :, c] = 0
    for c in (4, C - 5): P[:, :, c] = 0; P[:, :, c, K - 1] = WX - 1; s[:, :, c] = K - 1
    V[1::2, :, :, 0] = 512; V[0::2, :, :, 0] = 0
    return pack(X, V, P, s, w)
def setup_inputs_corners(rng):
    X, w, P, s = parts(rng); top = int(np.argmax(place(np.arange(4096))))
    for q in range(N):
        for g in range(8):
            z = (q + g) & 7
            if z == 2: w[q, g] = 0
            if z == 3: w[q, g] = 15
            if z == 4:
                w[q, g] = 15; w[q, g, 0] = 1; X[q, g, :, 0] = 0; X[q, g, :, WX - 1] = 0
                b = top // 15; X[q, g, 0, WX - 1] = top - 15 * b; X[q, g, 1, WX - 1] = min(b, 255); X[q, g, 2, WX - 1] = b - min(b, 255)
                P[q, g, C - 1] = 0; P[q, g, C - 1, 0] = WX - 1; s[q, g, C - 1] = 1; P[q, g, 0] = 0; P[q, g, C - 2] = 0
                e = rng.integers(1, WX - 1, 8); h = slots(prints(X[q, g:g + 1], np.repeat(e, K).reshape(1, 8, K)), w[q, g:g + 1])[1][0]
                P[q, g, 1] = int(e[np.argmax((h != 0) & (h != int(place(np.int64(top)))))])
            if z == 5: P[q, g] = rng.integers(0, WX, (C, 1))
            if z == 7: s[q, g] = rng.choice(np.array([0, 1, K - 1]), C)
    V = sow(rng, X, junk(rng, 0.2), w, P, s)
    for q in range(N):
        for g in range(8):
            z = (q + g) & 7
            if z == 0: V[q, g] = 512
            if z == 1: V[q, g] = np.where(V[q, g] == 512, rng.integers(0, 256, (16, WV)), V[q, g])
            if z == 2:
                P[q, g, :8] = int(rng.integers(0, WX))
                V[q, g][:, 0] = prints(X[q, g:g + 1], P[q, g:g + 1, :1])[0, :, 0]
            if z == 4:
                V[q, g][:, 0] = 512; V[q, g][:, int(place(np.int64(top)))] = 512
                F = prints(X[q, g:g + 1], P[q, g:g + 1, 1:2]); V[q, g][:, int(slots(F, w[q, g:g + 1])[1][0, 0])] = F[0, :, 0]
            if z == 5:
                F = prints(X[q, g:g + 1], P[q, g:g + 1]); h = slots(F, w[q, g:g + 1])[1]
                V[q, g][:, h[0]] = near(rng, F, 2, 12)[0]
            if z == 6:
                F = prints(X[q, g:g + 1], flip(P[q, g:g + 1], np.maximum(s[q, g:g + 1], 1)))[:, :, C >> 1:]; h = slots(F, w[q, g:g + 1])[1][:, :]
                o = np.argsort(rng.random(F.shape), axis=1)
                V[q, g][:, h[0]] = np.where(o < rng.integers(11, 13, (1, 1, F.shape[2])), F, 512)[0]
    return pack(X, V, P, s, w)
def setup_inputs_crowd(rng):
    X, w, P, s = parts(rng); V = junk(rng, 0.2); w[:, :, 3] = 1 + 2 * rng.integers(0, 8, (N, 8))
    for g in range(8):
        root = rng.integers(0, WX, K); m = int(rng.integers(1, K)); mc = rng.integers(1, K, (N, C))
        if g in (0, 2, 4): P[:, g] = root; s[:, g] = rng.integers(0, K, (N, C)) if g == 4 else m
        if g == 2: P[:, g, C - 1] = rng.integers(0, WX, K)
        if g == 3: P[:, g, 0::2] = root; P[:, g, 1::2] = flip(root, m); s[:, g] = m
        if g in (5, 7): P[:, g] = flip(np.broadcast_to(root, (N, C, K)), mc); s[:, g] = mc
        if g in (1, 6): P[:, g] = int(rng.integers(0, WX))
        if g == 6: P[:, g, 0] = rng.integers(0, WX, K)
        if g == 1:
            P[1::2, g] = rng.integers(0, WX, P[1::2, g].shape); s[1::2, g] = rng.integers(1, K, s[1::2, g].shape)
            for q in range(0, N, 2):
                r = (q - 1) % N; F = prints(X[q, g:g + 1], P[r, g:g + 1]); h = slots(F, w[q, g:g + 1])[1]
                V[q, g][:, h[0]] = near(rng, F, rng.integers(3, 6, (1, 1, C)), rng.integers(12, 17, (1, 1, C)))[0]
        if g == 2:
            for q in range(N):
                F = prints(X[q, g:g + 1], flip(np.broadcast_to(root, (1, K - 1, K)), np.arange(1, K)[None, :])); h = slots(F, w[q, g:g + 1])[1]
                V[q, g][:, h[0]] = near(rng, F, 5, 12)[0]
        if g in (1, 6, 7):
            for q in range(N):
                Q = root if g == 7 else P[0, g, C - 1]
                F = prints(X[q, g:g + 1], Q.reshape(1, 1, K)); h = int(slots(F, w[q, g:g + 1])[1][0, 0])
                V[q, g][:, h] = 512 if g == 1 and q & 1 else F[0, :, 0]
    return pack(X, V, P, s, w)
def setup_inputs_kin(rng):
    X, w, P, s = parts(rng)
    for q in range(1, N):
        o = rng.permutation(C); P[q] = P[0][:, o]; s[q] = s[0][:, o]
    return pack(X, np.full((N, 8, 16, WV), 512), P, s, w)
def check_inputs(d):
    bad = []
    for k, lo, hi in (("x", 0, 255), ("v", 0, 512), ("lanes", 0, WX - 1), ("s0", 0, K - 1), ("wt", 0, 15)):
        a = np.asarray(d[k]).astype(np.float64)
        if not np.all((a >= lo) & (a <= hi) & (a == np.floor(a))): bad.append("range of " + k)
    a = np.asarray(d["v"]).astype(np.float64)
    if np.any((a > 255) & (a < 512)): bad.append("v between 255 and 512")
    return bad
def visit(X, V, P, s, w, A):
    a = np.take_along_axis(X, P.reshape(8, 1, C * K), 2).reshape(8, 16, C, K); k = np.arange(K, dtype=np.int32)
    ak = np.add.accumulate(a * k, axis=3, dtype=np.int32); b = np.add.accumulate(a, axis=3, dtype=np.int32)
    F = np.ascontiguousarray(((ak[..., K - 1:] - 2 * ak + k * b) & 255)[..., 1:])
    u, h = slots(F.reshape(8, 16, C * (K - 1)), w)
    D = np.abs(np.take_along_axis(V, h[:, None, :], 2).reshape(F.shape) - F)
    u = u.reshape(8, C, K - 1); h = h.reshape(8, C, K - 1)
    close = D <= (2 + (A & 3)).reshape(8, 1, 1, 1)
    seen = np.add.reduce(close, axis=1, dtype=np.int32) >= TH
    far = np.add.reduce(D, axis=1, dtype=np.int32)
    i = np.argmin(np.where(seen, K, (np.arange(1, K) - s[:, :, None]) & (K - 1)), axis=2); go = np.logical_not(np.all(seen, axis=2))
    hc = np.take_along_axis(h, i[:, :, None], 2)[:, :, 0]; won = np.zeros((8, C), bool)
    for g in range(8):
        c = np.flatnonzero(go[g]); c = c[np.unique(hc[g, c], return_index=True)[1]]
        won[g, c] = True; V[g][:, hc[g, c]] = F[g][:, c, i[g, c]]
    su = np.take_along_axis(u, np.argmin(far, axis=2)[:, :, None], 2)[:, :, 0] & (K - 1)
    return np.where(won[:, :, None], flip(P, i + 1), P), np.where(won, s, su), C - np.add.reduce(won, axis=1, dtype=np.int64)
def reference(x, v, lanes, s0, wt):
    X = x.astype(np.float32).astype(np.int32).reshape(N, 8, 16, WX); V = v.astype(np.float32).astype(np.int32).reshape(N, 8, 16, WV)
    P = np.stack([gentries(a) for a in lanes]).astype(np.int64).reshape(N, 8, C, K); s = s0.astype(np.int64); w = wt.astype(np.int32).reshape(N, 8, 16)
    A = np.zeros((N, 8), np.int64)
    for t in range(RO):
        for q in range(N):
            r = (q - t) % N
            P[r], s[r], A[q] = visit(X[q], V[q], P[r], s[r], w[q], A[q])
    return {"yl": np.stack([gtable(a.reshape(8, C * K)) for a in P]).astype(np.float32), "ys": s.astype(np.float32), "yv": V.reshape(N, 128, WV).astype(np.float32).astype(BF)}

@@ -1,0 +1,476 @@
+from concourse.mybir import AluOpType as OP, AxisListType as AX, ActivationFunctionType as AF
+
+NCH = 3
+C, K, RO = 384, 8, 5
+NL = C // NCH
+CC = NL // 16
+M7 = 7 * CC
+G7 = (M7 + 15) // 16 * 16
+PC = NL // 2
+MB = 512 // NL
+NRAW = 2
+VW = 4096 + 2 * C + 16
+NOCOL = 4096
+NONE = float(2 ** 20 + NOCOL - 2048)
+
+SCRATCH = {
+    "xs": ("sbuf", [128, 4096], "bfloat16"), "vs": ("sbuf", [128, VW], "bfloat16"),
+    "cl": ("sbuf", [128, VW], "bfloat16"),
+    "lin": ("sbuf", [128, 192], "int32"), "wti": ("sbuf", [128, 4], "int32"), "s0i": ("sbuf", [128, C], "int32"),
+    "s0b": ("sbuf", [128, C], "bfloat16"),
+    "Lu": ("sbuf", [128, RO, 192], "uint16"), "Lo": ("sbuf", [128, RO, 192], "uint16"),
+    "Lf": ("sbuf", [128, 192], "float32"), "Lh": ("sbuf", [128, 192], "float32"),
+    "Sin": ("sbuf", [128, RO + 1, NCH * CC], "float32"), "OS": ("sbuf", [128, RO, NCH * CC], "float32"),
+    "shb": ("sbuf", [128, NCH * CC], "bfloat16"), "yst": ("sbuf", [128, C], "float32"),
+    "a": ("sbuf", [128, C * K], "bfloat16"), "a16": ("sbuf", [128, C * K], "float16"), "Q": ("sbuf", [128, NRAW, 512], "bfloat16"),
+    "F": ("sbuf", [128, NCH, 7 * NL], "bfloat16"), "D": ("sbuf", [128, NCH, 7 * NL], "float32"),
+    "R": ("sbuf", [128, NCH, 7 * NL], "bfloat16"), "E1": ("sbuf", [128, NCH, 7 * NL], "bfloat16"),
+    "Vg": ("sbuf", [128, NCH, 7 * NL], "bfloat16"), "big": ("sbuf", [128, 512], "bfloat16"),
+    "Xu": ("sbuf", [128, NCH, G7], "bfloat16"), "uf": ("sbuf", [128, NCH, G7], "float32"),
+    "sf": ("sbuf", [128, NCH, G7], "float32"), "m8": ("sbuf", [128, G7], "bfloat16"), "Fs": ("sbuf", [128, NCH, NL], "bfloat16"),
+    "eq": ("sbuf", [128, NCH * CC, NL], "bfloat16"), "clm": ("sbuf", [128, NCH, NL], "bfloat16"),
+    "tag": ("sbuf", [128, RO, NL], "bfloat16"),
+    "L16": ("sbuf", [128, NCH, PC], "float16"), "Y": ("sbuf", [128, NCH * 7, PC], "float16"),
+    "winP": ("sbuf", [128, NCH, PC], "bfloat16"), "dl": ("sbuf", [128, NCH, PC], "float32"),
+    "dw": ("sbuf", [128, NCH, PC], "float32"), "ln": ("sbuf", [128, NCH, PC], "float32"),
+    "ns": ("sbuf", [128, 32], "float32"), "pri": ("sbuf", [128, NCH * G7], "int32"),
+    "prj": ("sbuf", [128, NCH, G7], "int32"), "base": ("sbuf", [128, NCH, G7], "float32"),
+    "ui": ("sbuf", [128, NCH, G7], "int32"), "u": ("sbuf", [128, NCH, G7], "int32"),
+    "sq": ("sbuf", [128, NCH, G7], "int32"), "w37": ("sbuf", [128, NCH, G7], "int32"),
+    "sh": ("sbuf", [128, NCH, G7], "int32"), "hs": ("sbuf", [128, NCH, G7], "int32"),
+    "h": ("sbuf", [128, NCH, G7], "int32"), "h16": ("sbuf", [128, NCH, G7], "uint16"),
+    "u7": ("sbuf", [128, NCH, G7], "int32"), "P1": ("sbuf", [128, NCH, G7], "float32"),
+    "Kk": ("sbuf", [128, NCH, 8 * CC], "float32"), "K4": ("sbuf", [128, NCH, 4 * CC], "float32"),
+    "K2": ("sbuf", [128, NCH, 2 * CC], "float32"), "K1": ("sbuf", [128, NCH, 16], "float32"),
+    "Kb": ("sbuf", [128, NCH, 8 * CC], "float32"), "Kb4": ("sbuf", [128, NCH, 4 * CC], "float32"),
+    "Kb2": ("sbuf", [128, NCH, 2 * CC], "float32"),
+    "X": ("sbuf", [128, NCH, 16], "bfloat16"), "hn16": ("sbuf", [128, NCH, 16], "float16"),
+    "hn32": ("sbuf", [128, NCH, 16], "float32"), "co": ("sbuf", [128, NCH, 16], "uint16"),
+    "sel": ("sbuf", [128, NCH, G7], "bfloat16"), "selc": ("sbuf", [128, NCH, G7], "bfloat16"),
+    "fo": ("sbuf", [128, NCH, 16], "uint16"), "k2i": ("sbuf", [128, NCH * CC], "int32"),
+    "ds": ("sbuf", [128, NCH * CC], "int32"), "pre": ("sbuf", [128, NCH, 16], "float32"),
+    "sd": ("sbuf", [128, 2, NCH * CC], "float32"), "pw": ("sbuf", [128, NCH, 16], "float32"), "vo": ("sbuf", [128, NCH, 16], "uint16"),
+    "wab": ("sbuf", [128, NCH * CC], "bfloat16"),
+    "cn": ("sbuf", [128, 8], "float32"), "cni": ("sbuf", [128, 8], "int32"), "tol": ("sbuf", [128, RO, 4], "float32"),
+    "one": ("sbuf", [128, 2048], "bfloat16"), "cI": ("sbuf", [128, 8, 128], "bfloat16"),
+    "Zs": ("sbuf", [128, 5, 144], "bfloat16"), "Z2": ("sbuf", [128, 144], "bfloat16"), "Z3": ("sbuf", [128, 144], "bfloat16"),
+    "SI": ("sbuf", [128, 16 * 128], "bfloat16"), "MP": ("sbuf", [128, 8, 128], "bfloat16"),
+    "OPm": ("sbuf", [128, 6, 128], "bfloat16"), "PM": ("sbuf", [128, 7, 128], "bfloat16"), "Bk": ("sbuf", [128, 128], "bfloat16"),
+    "ti": ("sbuf", [128, 4, 144], "int32"), "tf": ("sbuf", [128, 4, 144], "float32"),
+    "pc": ("sbuf", [128, 8], "int32"), "pf": ("sbuf", [128, 16], "float32"),
+    "thr": ("sbuf", [128, PC], "float32"), "mpat": ("sbuf", [128, NCH * G7], "int32"), "ccp": ("sbuf", [128, 16], "bfloat16"),
+    "dm": ("sbuf", [128, NCH * CC], "float16"), "bl": ("sbuf", [128, 16], "uint16"),
+}
+for _b in range(8):
+    SCRATCH["ps%d" % _b] = ("psum", [128, 512], "float32")
+
+LOADS = ["dx", "dv", "dl", "dw", "ds"]
+SEMAPHORES = ["eV", "eA", "eP", "eG", "sent", "out"] + LOADS
+SEMAPHORES += ["rl%d_%d" % (t, c) for t in range(1, RO + 1) for c in range(NCH)]
+SEMAPHORES += ["rs%d" % t for t in range(1, RO + 1)]
+
+G1V = ()
+SEED = 1
+JIT = 0.0
+RACT = 7
+CY, PCY, HOP, NET, LOOK, PIECE = 0.001, 0.0005, 0.12, 3.0, 0.05, 0.25
+
+
+def coef(m, k):
+    return m - k if k <= m else k
+
+
+def build(g, T, topo, core, rank):
+    n = len(T.cores)
+    ops = []
+    lastw, readers, bank = {}, {}, {}
+    V, A, PE = g.vector, g.scalar, g.tensor
+
+    def op(q, calls, dur, r=(), w=(), b=(), sem=None, ext=(), after=()):
+        i = len(ops)
+        deps = set()
+        for x in r:
+            if x in lastw: deps.add(lastw[x])
+        for x in w:
+            if x in lastw: deps.add(lastw[x])
+            deps.update(readers.get(x, ()))
+        for x in r: readers.setdefault(x, []).append(i)
+        for x in w:
+            lastw[x] = i; readers[x] = []
+        deps.discard(i)
+        ops.append([q, calls if isinstance(calls, list) else [calls], dur, deps, sem, list(ext), list(after), list(b), (list(w) + [""])[0]])
+        return i
+
+    def vd(nel, f=1.0): return 0.05 + max(64, nel * f) * CY
+    def ts(out, in0, s1, s2, o0, o1, nel, r, w, b=(), f=1.0, ext=(), after=()):
+        if o1 is None: fn = lambda: V.tensor_scalar(out, in0, s1, None, o0)
+        else: fn = lambda: V.tensor_scalar(out, in0, s1, s2, o0, o1)
+        return op("V", fn, vd(nel, f), r, w, b, ext=ext, after=after)
+    def tt(out, in0, in1, o, nel, r, w, b=(), f=2.0, ext=(), after=()):
+        return op("V", lambda: V.tensor_tensor(out, in0, in1, o), vd(nel, f), r, w, b, ext=ext, after=after)
+    def cp(out, in_, nel, r, w, b=(), f=1.0):
+        return op("V", lambda: V.tensor_copy(out, in_), vd(nel, f), r, w, b)
+    def ms(out, c, nel, w):
+        return op("V", lambda: V.memset(out, c), vd(nel, 0.5), (), w)
+    def act(out, in_, fn, bias, scale, nel, r, w, b=(), f=1.0, ext=(), after=()):
+        return op("A", lambda: A.activation(out, in_, fn, bias=bias, scale=scale), vd(nel, f) + 0.02, r, w, b, ext=ext, after=after)
+    def mm(lst, r, w, b, first=True, last=True, group=True):
+        cut = 0; tot = 0
+        for j, x in enumerate(lst):
+            tot += max(64, x[3]) * PCY
+            if (b[0] < NRAW or not group) and tot > PIECE and j >= 1 and len(lst) - j >= 2:
+                cut = j; break
+        if cut:
+            mm(lst[:cut], r, w, b, first, False, group)
+            return mm(lst[cut:], r, w, b, False, last, group)
+        calls = []; dur = 0.02
+        for j, (o, l, x, nn) in enumerate(lst):
+            st = (first and j == 0) if group else True
+            sp = (last and j == len(lst) - 1) if group else True
+            calls.append(lambda o=o, l=l, x=x, st=st, sp=sp: PE.matmul(o, l, x, st, sp))
+            dur += max(64, nn) * PCY
+        return op("P", calls, dur, r, w, b)
+    def io(out, pat, base, cm, nel, w, small=False):
+        if small: fn = lambda: g.iota(out, pat, base, cm, allow_small_or_imprecise_dtypes=True)
+        else: fn = lambda: g.iota(out, pat, base, cm)
+        return op("G", fn, 0.15 + 2 * nel * CY, (), w)
+    def sel_(out, in_, pat, cmp, base, cm, nel, r, w):
+        return op("G", lambda: g.affine_select(out, in_, pat, cmp, 0.0, base, cm), 0.2 + 2 * nel * CY, r, w)
+    def dma(out, in_, dur, r, w, sem, ext=(), after=()):
+        return op("S", lambda: g.sync.dma_start(out, in_), dur, r, w, sem=(sem, 16), ext=ext, after=after)
+    def send(dst, out, in_, rs, r):
+        rid, pid, _ = topo.addr(dst); mask = topo.mask(core, dst)
+        ne = len(topo.engines(core, dst))
+        return op("G", lambda: g.remote_dma(out, in_, T.sem[rs], T.sem.sent, pid, rid, mask), 0.6, r, (), sem=("sent", -ne))
+    def arrival(src, rs):
+        return (rs, len(topo.engines(src, core)))
+    ps = [T["ps%d" % i] for i in range(8)]
+    PU, PT, PH = ps[5], ps[6], ps[7]
+
+    dma(T.lin[:], T.lanes[:], 2.0, (), ["lin"], "dl")
+    dma(T.xs[:], T.x[:], 5.0, (), ["xs"], "dx")
+    dma(T.wti[:, 0:1], T.wt[:], 2.0, (), ["wti"], "dw")
+    dma(T.s0i[0:8, :], T.s0[:], 2.0, (), ["s0i"], "ds")
+    dma(T.vs[:, 0:4096], T.v[:], 8.0, (), ["vs"], "dv")
+
+    ms(T.one[:, 0:144], 1.0, 144, ["one"])
+    sel_(T.cI[:, 1, :], T.one[:, 0:128], [[-1, 128]], OP.is_equal, 0, 1, 128, ["one"], ["I1"])
+    for c in range(2, 8):
+        act(T.cI[:, c, :], T.cI[:, 1, :], AF.Identity, 0.0, float(c), 128, ["I1"], ["I%d" % c])
+    act(T.cI[:, 0, :], T.cI[:, 1, :], AF.Identity, 0.0, -1.0, 128, ["I1"], ["I0"])
+    cIall = ["I%d" % c for c in range(8)]
+    io(T.pc[:, 0:1], [[0, 1]], 0, 1, 1, ["pc0"])
+    for j, (mk, nm) in enumerate(((112, "g16"), (15, "r"), (7, "k"), (8, "pb"))):
+        ts(T.pc[:, 1 + j:2 + j], T.pc[:, 0:1], mk, None, OP.bitwise_and, None, 1, ["pc0"], ["pc" + nm])
+    cp(T.pf[:, 0:4], T.pc[:, 1:5], 4, ["pcg16", "pcr", "pck", "pcpb"], ["pf"])
+    cp(T.pf[:, 4:5], T.wti[:, 0:1], 1, ["wti"], ["wf"])
+    ts(T.pf[:, 6:7], T.pf[:, 1:2], float(-NL), None, OP.add, None, 1, ["pf"], ["pf6"])
+    io(T.tf[:, 0, :], [[1, 144]], -15, 0, 144, ["tf0"], True)
+    ts(T.Zs[:, 0, :], T.tf[:, 0, :], T.pf[:, 0:1], T.pf[:, 4:5], OP.is_equal, OP.mult, 144, ["tf0", "pf", "wf"], ["ZW"])
+    for j, wgt in ((1, 2.0 ** 22), (2, 64.0)):
+        ts(T.Zs[:, j, :], T.tf[:, 0, :], T.pf[:, 0:1], wgt, OP.is_equal, OP.mult, 144, ["tf0", "pf"], ["Z%d" % j])
+    sel_(T.Z3[0:8, :], T.one[0:8, 0:144], [[1, 144]], OP.is_equal, -15, -16, 144, ["one"], ["Z3s"])
+    io(T.mpat[:], [[0, NCH], [4096, G7 // CC], [0, CC]], 4096 + 2 ** 19 + 2048, 0, NCH * G7, ["mp0"])
+    io(T.m8[:, 0:M7], [[8, 7], [0, CC]], 8, 0, M7, ["m8"], True)
+    nb = G7 // 16
+    io(T.ti[:, 0, 0:nb], [[16, nb]], 0, 0, nb, ["b0"])
+    ts(T.ti[:, 1, 0:nb], T.ti[:, 0, 0:nb], T.pf[:, 1:2], None, OP.add, None, nb, ["b0", "pf"], ["b1"])
+    ts(T.ti[:, 2, 0:nb], T.ti[:, 1, 0:nb], float(65536 // CC + 1), None, OP.mult, None, nb, ["b1"], ["b2"])
+    ts(T.ti[:, 3, 0:nb], T.ti[:, 2, 0:nb], 16, None, OP.arith_shift_right, None, nb, ["b2"], ["b3"])
+    ts(T.ti[:, 2, 0:nb], T.ti[:, 3, 0:nb], float(-CC), None, OP.mult, None, nb, ["b3"], ["b2"])
+    tt(T.ti[:, 3, 0:nb], T.ti[:, 2, 0:nb], T.ti[:, 1, 0:nb], OP.add, nb, ["b2", "b1"], ["b3"])
+    for c in range(NCH):
+        ts(T.bl[:, c * nb:(c + 1) * nb], T.ti[:, 3, 0:nb], float(c * CC), None, OP.add, None, nb, ["b3", "bl"], ["bl"])
+    ms(T.Kk[:], NONE, NCH * 8 * CC, ["Kk%d" % c for c in range(NCH)])
+    ms(T.Kb[:], NONE, NCH * 8 * CC, ["Kb"])
+    ms(T.P1[:], -1.0, NCH * G7, ["P1_%d" % c for c in range(NCH)])
+    ms(T.ns[:], 0.0, 32, ["ns"])
+    ms(T.K1[:], 0.0, NCH * 16, ["K1_%d" % c for c in range(NCH)])
+    ms(T.tol[:, 0, 0:1], 2.0 - 256, 1, ["tol0a"]); ms(T.big[:], 33024.0, 512, ["big"])
+    ms(T.one[:, 144:2048], 1.0, 1904, ["oneb"])
+    for hf in range(2):
+        sel_(T.SI[:, 1024 * hf:1024 * (hf + 1)], T.one[:, 0:1024], [[-1, 8], [-16, 8], [0, 16]], OP.is_equal, -8 * hf, 1, 1024, ["one", "oneb"], ["SI%d" % hf])
+    for rh in range(8):
+        sel_(T.MP[:, rh, :], T.one[:, 0:128], [[-16, 8], [-1, 2], [0, 8]], OP.is_equal, -2 * rh, 1, 128, ["one"], ["MP%d" % rh])
+    MPall = ["MP%d" % rh for rh in range(8)]
+    ms(T.tf[:, 1, 0:16], 0.5, 16, ["hf"]); ms(T.tf[:, 1, 16:32], 0.0, 16, ["zf"])
+    op("V", lambda: V.tensor_tensor_scan(T.tf[:, 1, 32:48], T.tf[:, 1, 0:16], T.tf[:, 1, 16:32], 65536.0, OP.mult, OP.add), vd(16), ["hf", "zf"], ["pw2"])
+    ts(T.tf[:, 1, 48:64], T.tf[:, 0, 15:31], T.pf[:, 1:2], None, OP.is_equal, None, 16, ["tf0", "pf"], ["dg"])
+    tt(T.tf[:, 1, 64:80], T.tf[:, 1, 48:64], T.tf[:, 1, 32:48], OP.mult, 16, ["dg", "pw2"], ["dg2"])
+    op("V", lambda: V.tensor_reduce(T.pf[:, 5:6], T.tf[:, 1, 64:80], AX.X, OP.add), vd(16), ["dg2"], ["pf5"])
+    io(T.tf[:, 2, 0:128], [[16, 8], [0, 16]], 0, 0, 128, ["tf2"], True)
+    ts(T.Bk[:], T.tf[:, 2, 0:128], T.pf[:, 0:1], None, OP.is_equal, None, 128, ["tf2", "pf"], ["Bk"])
+    io(T.tf[:, 3, 0:128], [[16, 8], [8, 2], [0, 8]], 0, 0, 128, ["tf3"], True)
+    ts(T.pf[:, 8:9], T.pf[:, 0:1], 8.0, None, OP.add, None, 1, ["pf"], ["pf8"])
+    for p in range(2):
+        col = T.pf[:, 0:1] if p == 0 else T.pf[:, 8:9]
+        ts(T.OPm[:, p, :], T.tf[:, 3, 0:128], col, 65536.0, OP.is_equal, OP.mult, 128, ["tf3", "pf", "pf8"], ["OA%d" % p])
+        ts(T.OPm[:, 2 + p, :], T.tf[:, 3, 0:128], col, T.pf[:, 5:6], OP.is_equal, OP.mult, 128, ["tf3", "pf", "pf8", "pf5"], ["OD%d" % p])
+    ts(T.pf[:, 9:10], T.pf[:, 3:4], -1.0 / 16, 1.0, OP.mult, OP.add, 1, ["pf"], ["pf9"])
+    for rh in range(8):
+        ms(T.thr[:, rh:PC:8], 2.0 ** (16 - 2 * rh), CC, ["th%d" % rh])
+    ts(T.thr[:], T.thr[:], T.pf[:, 9:10], -0.5, OP.mult, OP.add, PC, ["pf9"] + ["th%d" % rh for rh in range(8)], ["thr"])
+    ts(T.pf[:, 10:11], T.pf[:, 3:4], 0.125, T.pf[:, 0:1], OP.mult, OP.add, 1, ["pf"], ["pf10"])
+    ts(T.pf[:, 11:12], T.pf[:, 2:3], 1000.0, T.pf[:, 10:11], OP.mult, OP.add, 1, ["pf", "pf10"], ["pf11"])
+    ts(T.Z2[:], T.tf[:, 0, :], T.pf[:, 11:12], -8192.0, OP.is_equal, OP.mult, 144, ["tf0", "pf11"], ["Z2s"])
+    io(T.tf[:, 2, 0:128], [[64, 16], [1, 8]], 0, 0, 128, ["tf2"], True)
+    ts(T.pf[:, 12:13], T.pf[:, 0:1], T.pf[:, 3:4], -8.0, OP.add, OP.mult, 1, ["pf"], ["pf12"])
+    ts(T.pf[:, 13:14], T.pf[:, 12:13], T.pf[:, 2:3], None, OP.add, None, 1, ["pf", "pf12"], ["pf13"])
+    ts(T.tf[:, 3, 0:128], T.tf[:, 2, 0:128], T.pf[:, 13:14], None, OP.add, None, 128, ["tf2", "pf13"], ["tf3"])
+    for m in range(1, 8):
+        j = 4 + (m & 1)
+        sel_(T.OPm[:, j, :], T.cI[:, 1, :], [[0, 16], [-1, 8]], OP.is_ge, m, 0, 128, ["I1"], ["tm%d" % j])
+        ts(T.PM[:, m - 1, :], T.tf[:, 3, 0:128], float(m), None, OP.is_equal, None, 128, ["tf3"], ["PM%d" % m])
+        tt(T.PM[:, m - 1, :], T.PM[:, m - 1, :], T.OPm[:, j, :], OP.subtract, 128, ["tm%d" % j, "PM%d" % m], ["PM%d" % m])
+    PMall = ["PM%d" % m for m in range(1, 8)]
+    io(T.ccp[:, 0:CC], [[1, CC]], 0, 0, CC, ["ccp"], True)
+    io(T.ti[:, 0, 32:32 + NCH * CC], [[16, NCH * CC]], 1025, 0, NCH * CC, ["d0"])
+    ts(T.dm[:], T.ti[:, 0, 32:32 + NCH * CC], T.pf[:, 1:2], 2.0, OP.add, OP.mult, NCH * CC, ["d0", "pf"], ["dm"])
+    for j in range(0, NOCOL, 1024):
+        ms(T.cl[:, j:j + 1024], 0.0, 1024, ["cl"])
+    ms(T.cl[:, NOCOL:VW], 64.0, VW - NOCOL, ["cl"])
+    ms(T.vs[:, 4096:VW], 0.0, VW - 4096, ["vsb"])
+    for t in range(RO):
+        ms(T.tag[:, t, :], float(t + 1), NL, ["tag%d" % t])
+    for c in range(NCH):
+        cp(T.Lu[:, 0, c * PC:(c + 1) * PC], T.lin[:, c * PC:(c + 1) * PC], PC, ["lin"], ["Lu0_%d" % c])
+    cp(T.s0b[0:8, :], T.s0i[0:8, :], C, ["s0i"], ["s0b"])
+    mm([(PU[:, 200:200 + NCH * CC], T.Z3[0:8, 15 - r:143 - r], T.s0b[0:8, r:C:16], NCH * CC) for r in range(16)], ["Z3s", "s0b"], ["pS"], [5])
+    act(T.Sin[:, 0, :], PU[:, 200:200 + NCH * CC], AF.Identity, 0.0, 1.0, NCH * CC, ["pS"], ["Sin0"], [5])
+
+    nxt = T.cores[(rank + 1) % n]; prv = T.cores[(rank - 1) % n]
+    home = T.cores[(rank - (RO - 1)) % n]; last = T.cores[(rank + RO - 1) % n]
+    sends = {}
+    rot = [0, 0]
+
+    def phase_x(t, c):
+        s = "%d" % c
+        Lu = T.Lu[:, t, c * PC:(c + 1) * PC]
+        el = [arrival(prv, "rl%d_%d" % (t, c))] if t else []
+        al = [sends["l", t - 1, c]] if t else []
+        a0 = c * NL * K
+        onv = c in G1V
+        Ta = T.a16 if onv else T.a
+        if onv:
+            ts(Ta[:, a0:a0 + NL * K], T.xs[:].indirect(Lu), 1280.0, None, OP.add, None, NL * K, ["xs", "Lu%d_%d" % (t, c)], ["a" + s], f=1.56, ext=el, after=al)
+        else:
+            act(Ta[:, a0:a0 + NL * K], T.xs[:].indirect(Lu), AF.Identity, 0.0, 1.0, NL * K, ["xs", "Lu%d_%d" % (t, c)], ["a" + s], f=1.56, ext=el, after=al)
+        ts(T.L16[:, c, :], Lu, -2048.0, None, OP.add, None, PC, ["Lu%d_%d" % (t, c)], ["L16" + s], f=0.5, ext=el, after=al)
+        if c == 0:
+            es = [arrival(prv, "rs%d" % t)] if t else []
+            as_ = [sends["s", t - 1]] if t else []
+            act(T.ns[:, 0:NCH * CC], T.Sin[:, t, :], AF.Identity, 32768.0, -4096.0, NCH * CC, ["Sin%d" % t], ["ns", "sarr"], ext=es, after=as_)
+            tt(T.pri[:], T.ns[:].indirect(T.bl[:, 0:NCH * nb]), T.mpat[:], OP.add, NCH * G7, ["ns", "bl", "mp0"], ["pri"], f=1.56)
+            ts(T.prj[:], T.pri[:], 2 ** 19 + 7 * 4096 + 2048, None, OP.bitwise_and, None, NCH * G7, ["pri"], ["base"])
+        Fall = []
+        for m0 in range(1, 8, MB):
+            mlist = list(range(m0, min(8, m0 + MB))); w_ = len(mlist) * NL
+            bk = rot[0] % NRAW; rot[0] += 1
+            lst = [] if onv else [(ps[bk][:, 0:w_], T.cI[:, 1, :], T.big[:, 0:w_], w_)]
+            for j, m in enumerate(mlist):
+                for k in range(K):
+                    if coef(m, k):
+                        lst.append((ps[bk][:, j * NL:(j + 1) * NL], T.cI[:, coef(m, k), :], Ta[:, a0 + k:a0 + NL * K:K], NL))
+            mm(lst, ["a" + s, "big"] + cIall, ["raw%d" % bk, "turn"], [bk])
+            act(T.Q[:, bk, 0:w_], ps[bk][:, 0:w_], AF.Identity, -127.5, 1.0, w_, ["raw%d" % bk], ["Q%d" % bk], [bk])
+            tt(T.F[:, c, (m0 - 1) * NL:(m0 - 1) * NL + w_], ps[bk][:, 0:w_], T.Q[:, bk, 0:w_], OP.subtract, w_, ["raw%d" % bk, "Q%d" % bk], ["F%s_%d" % (s, m0)], [bk], f=1)
+            Fall.append("F%s_%d" % (s, m0))
+        mm([(PU[:, 0:M7], T.Zs[:, 0, 15 - r:143 - r], T.F[:, c, r:7 * NL:16], M7) for r in range(16)], Fall + ["ZW"], ["pu"], [5])
+        S7 = slice(0, M7); C0 = 2 ** 19 + 4096
+        act(T.Xu[:, c, S7], PU[:, 0:M7], AF.Identity, C0 - 2047.5, 1.0, M7, ["pu"], ["Xu" + s], [5])
+        tt(T.uf[:, c, S7], PU[:, 0:M7], T.Xu[:, c, S7], OP.subtract, M7, ["pu", "Xu" + s], ["uf" + s], [5], f=1)
+        act(T.sf[:, c, S7], T.uf[:, c, S7], AF.Square, C0 + 592.0, 1.0, M7, ["uf" + s], ["sf" + s])
+        ts(T.sq[:, c, S7], T.sf[:, c, S7], -592.0 * 592, None, OP.add, None, M7, ["sf" + s], ["sq" + s])
+        ts(T.h[:, c, S7], T.sq[:, c, S7], 5, 4095, OP.arith_shift_right, OP.bitwise_and, M7, ["sq" + s], ["h" + s])
+        cp(T.h16[:, c, S7], T.h[:, c, S7], M7, ["h" + s], ["h16" + s])
+        tt(T.P1[:, c, S7], T.prj[:, c, S7], T.h[:, c, S7], OP.add, M7, ["base", "h" + s], ["P1_" + s])
+        if c == NCH - 1:
+            cp(T.ui[:, :, S7], T.uf[:, :, S7], NCH * M7, ["uf%d" % j for j in range(NCH)], ["ui"])
+            ts(T.u7[:, :, S7], T.ui[:, :, S7], 7, None, OP.bitwise_and, None, NCH * M7, ["ui"], ["u7"])
+        return Fall
+
+    def phase_y(t, c, Fall):
+        s = "%d" % c; W = 7 * NL
+        Eall, Rall = [], []
+        for m0 in range(0, 7, MB):
+            m1 = min(7, m0 + MB); w_ = (m1 - m0) * NL; cs = slice(m0 * NL, m1 * NL); x = "%s_%d" % (s, m0)
+            bk = NRAW + rot[1] % 2; rot[1] += 1
+            act(T.Vg[:, c, cs], T.vs[:, 0:4096].indirect(T.h16[:, c, m0 * CC:m1 * CC]), AF.Identity, 0.0, 1.0, w_, ["vs", "h16" + s], ["Vg" + x], f=1.56)
+            mm([(ps[bk][:, 0:w_], T.cI[:, 0, :], T.F[:, c, cs], w_), (ps[bk][:, 0:w_], T.cI[:, 1, :], T.Vg[:, c, cs], w_)], ["Vg" + x] + Fall, ["raw%d" % bk], [bk])
+            act(T.D[:, c, cs], ps[bk][:, 0:w_], AF.Abs, 0.0, 1.0, w_, ["raw%d" % bk], ["D" + x], [bk])
+            if m0 < RACT: act(T.R[:, c, cs], T.D[:, c, cs], AF.Identity, -256.0, 1.0, w_, ["D" + x], ["R" + x])
+            else: ts(T.R[:, c, cs], T.D[:, c, cs], -256.0, None, OP.add, None, w_, ["D" + x], ["R" + x])
+            ts(T.E1[:, c, cs], T.R[:, c, cs], T.tol[:, t, 0:1], -23.0 / 32, OP.is_le, OP.add, w_, ["R" + x, "tol%da" % t], ["E" + x], f=0.5)
+            Eall.append("E" + x); Rall.append("R" + x)
+        def sums(out, B, j):
+            return [(out, T.Zs[:, j, 15 - r:143 - r], B[:, c, r:W:16], M7) for r in range(16)]
+        mm(sums(PT[:, 0:M7], T.E1, 1), Eall + ["Z1"], ["pT"], [6])
+        PF = PU[:, 256 + c * M7:256 + (c + 1) * M7]
+        mm(sums(PF, T.R, 2) + [(PF, T.cI[:, 1, :], T.m8[:, 0:M7], M7)], Rall + ["Z2", "m8"], ["pfar" + s], [5])
+        tt(T.Kk[:, c, CC:8 * CC], PT[:, 0:M7], T.P1[:, c, 0:M7], OP.max, M7, ["pT", "P1_" + s], ["Kk" + s], [6], f=1)
+        tt(T.K4[:, c, :], T.Kk[:, c, 0:4 * CC], T.Kk[:, c, 4 * CC:8 * CC], OP.min, 4 * CC, ["Kk" + s], ["K4" + s])
+        tt(T.K2[:, c, :], T.K4[:, c, 0:2 * CC], T.K4[:, c, 2 * CC:4 * CC], OP.min, 2 * CC, ["K4" + s], ["K2" + s])
+        tt(T.K1[:, c, 0:CC], T.K2[:, c, 0:CC], T.K2[:, c, CC:2 * CC], OP.min, CC, ["K2" + s], ["K1_" + s])
+        Km = T.K1[:, c, 0:CC]
+        ts(T.X[:, c, 0:CC], Km, 0.5, None, OP.add, None, CC, ["K1_" + s], ["X" + s])
+        tt(T.hn16[:, c, 0:CC], Km, T.X[:, c, 0:CC], OP.subtract, CC, ["K1_" + s, "X" + s], ["hn16" + s])
+        tt(T.hn32[:, c, 0:CC], Km, T.X[:, c, 0:CC], OP.subtract, CC, ["K1_" + s, "X" + s], ["hn32" + s])
+        mm([(PH[:, r:NL:16], T.SI[:, 128 * r:128 * (r + 1)], T.hn16[:, c, 0:CC], CC) for r in range(16)], ["hn16" + s, "SI0", "SI1"], ["pH"], [7], group=False)
+        ts(T.co[:, c, 0:CC], T.hn32[:, c, 0:CC], 2048.0, None, OP.add, None, CC, ["hn32" + s], ["co" + s])
+        act(T.clm[:, c, :], T.cl[:].indirect(T.co[:, c, 0:CC]), AF.Relu, float(-t), 1.0, NL, ["cl", "clb", "co" + s], ["clm" + s], f=1.56)
+        e0 = c * CC
+        for j in range(CC):
+            ts(T.eq[:, e0 + j, 0:NL - 16 * j], PH[:, 16 * j:NL], T.hn32[:, c, j:j + 1], None, OP.is_equal, None, NL - 16 * j, ["pH", "hn32" + s], ["eq%s_%d" % (s, j)], [7])
+        PL = PH[:, 256:256 + PC]
+        lst = []
+        for p in range(2):
+            lst.append((PL, T.OPm[:, p, :], T.clm[:, c, p:NL:2], PC))
+            lst.append((PL, T.OPm[:, 2 + p, :], T.eq[:, e0:e0 + CC, p:16:2], PC))
+            for j in range(CC - 1):
+                lst.append((PH[:, 256 + 8 * (j + 1):256 + PC], T.OPm[:, p, :], T.eq[:, e0 + j, 16 + p:NL - 16 * j:2], PC - 8 * (j + 1)))
+        mm(lst, ["clm" + s, "OA0", "OA1", "OD0", "OD1"] + ["eq%s_%d" % (s, j) for j in range(CC)], ["pL"], [7])
+        tt(T.sel[:, c, :], T.K1[:, c, :].indirect(T.bl[:, 0:nb]), T.P1[:, c, :], OP.is_equal, G7, ["K1_" + s, "bl", "P1_" + s], ["sel" + s], f=1.56)
+        mper = 512 // PC
+        for bi, m0 in enumerate(range(0, 7, mper if 7 * PC <= 512 else 4)):
+            m1 = min(7, m0 + (mper if 7 * PC <= 512 else 4)); bk = 4; bi = 0
+            mm([(ps[bk][:, rh:(m1 - m0) * PC:8], T.MP[:, rh, :], T.sel[:, c, m0 * CC:m1 * CC], (m1 - m0) * CC) for rh in range(8)], ["sel" + s] + MPall, ["pM%d" % bi], [bk], group=False)
+            for m in range(m0, m1):
+                tt(T.Y[:, c * 7 + m, :], ps[bk][:, (m - m0) * PC:(m - m0 + 1) * PC], T.L16[:, c, :], OP.mult, PC, ["pM%d" % bi, "L16" + s], ["Y%s_%d" % (s, m)], [bk], f=1)
+        PD = PT[:, 256:256 + PC]
+        mm([(PD, T.PM[:, m, :], T.Y[:, c * 7 + m, :], PC) for m in range(7)], PMall + ["Y%s_%d" % (s, m) for m in range(7)], ["pD"], [6])
+        tt(T.winP[:, c, :], PL, T.thr[:], OP.is_lt, PC, ["pL", "thr"], ["winP" + s], [7], f=1)
+        tt(T.dw[:, c, :], PD, T.winP[:, c, :], OP.mult, PC, ["pD", "winP" + s], ["dw" + s], [6], f=1)
+        tt(T.ln[:, c, :], T.dw[:, c, :], T.L16[:, c, :], OP.add, PC, ["dw" + s, "L16" + s], ["ln" + s])
+        cs = slice(c * PC, (c + 1) * PC)
+        if t < RO - 1:
+            ts(T.Lo[:, t, cs], T.ln[:, c, :], 2048.0, None, OP.add, None, PC, ["ln" + s], ["Lo%d_%d" % (t, c)])
+            sends["l", t, c] = send(nxt, T.Lu[:, t + 1, cs], T.Lo[:, t, cs], "rl%d_%d" % (t + 1, c), ["Lo%d_%d" % (t, c)])
+        else:
+            ts(T.Lf[:, cs], T.ln[:, c, :], 2048.0, None, OP.add, None, PC, ["ln" + s], ["Lf" + s])
+            sends["l", t, c] = send(home, T.Lh[:, cs], T.Lf[:, cs], "rl%d_%d" % (t + 1, c), ["Lf" + s])
+        act(T.selc[:, c, 0:M7], T.sel[:, c, 0:M7], AF.Identity, 0.0, float(CC), M7, ["sel" + s], ["selc" + s])
+        PP = PU[:, 128:128 + CC]
+        mm([(PP, T.cI[:, m, :], T.selc[:, c, (m - 1) * CC:m * CC], CC) for m in range(1, 8)] + [(PP, T.cI[:, 1, :], T.ccp[:, 0:CC], CC)], ["selc" + s, "ccp"], ["pP"], [5])
+        ts(T.fo[:, c, 0:CC], PP, 16.0, T.pf[:, 6:7], OP.mult, OP.add, CC, ["pP", "pf6"], ["fo" + s], [5])
+        act(T.Fs[:, c, :], T.F[:, c, :].indirect(T.fo[:, c, 0:CC]), AF.Identity, 0.0, 1.0, NL, ["fo" + s] + Fall, ["Fs" + s], f=1.56)
+        PW = PH[:, 400 + c * CC:400 + (c + 1) * CC]
+        mm([(PW, T.cI[:, 1, :], T.dm[:, c * CC:(c + 1) * CC], CC)] + [(PW, T.Z2[:, 15 - 2 * rh:143 - 2 * rh], T.winP[:, c, rh:PC:8], CC) for rh in range(8)], ["winP" + s, "Z2s", "dm"], ["pW" + s], [7])
+        tt(T.pw[:, c, 0:CC], PW, T.hn32[:, c, 0:CC], OP.max, CC, ["pW" + s, "hn32" + s], ["pw" + s], [7], f=1)
+        ts(T.vo[:, c, 0:CC], T.pw[:, c, 0:CC], 2048.0, None, OP.add, None, CC, ["pw" + s], ["vo" + s])
+        if c < NCH - 1:
+            cp(T.cl[:, 0:VW].indirect(T.vo[:, c, 0:CC]), T.tag[:, t, :], NL, ["vo" + s, "tag%d" % t], ["cl"], f=3.8)
+
+    NC_ = NCH * CC
+    for t in range(RO):
+        Fs_ = [phase_x(t, c) for c in range(NCH)]
+        for c in range(NCH): phase_y(t, c, Fs_[c])
+        for c in range(NCH):
+            cp(T.vs[:].indirect(T.vo[:, c, 0:CC]), T.Fs[:, c, :], NL, ["vo%d" % c, "Fs%d" % c, "vsb"], ["vs"], f=3.8)
+        tt(T.Kb[:, :, CC:8 * CC], PU[:, 256:256 + NCH * M7], T.u7[:, :, 0:M7], OP.add, NCH * M7, ["pfar%d" % c for c in range(NCH)] + ["u7"], ["Kb"], [5], f=1)
+        tt(T.Kb4[:], T.Kb[:, :, 0:4 * CC], T.Kb[:, :, 4 * CC:8 * CC], OP.min, 4 * NC_, ["Kb"], ["Kb4"])
+        tt(T.Kb2[:], T.Kb4[:, :, 0:2 * CC], T.Kb4[:, :, 2 * CC:4 * CC], OP.min, 2 * NC_, ["Kb4"], ["Kb2"])
+        tt(T.k2i[:], T.Kb2[:, :, 0:CC], T.Kb2[:, :, CC:2 * CC], OP.min, NC_, ["Kb2"], ["k2i"])
+        ts(T.ds[:], T.k2i[:], 7, None, OP.bitwise_and, None, NC_, ["k2i"], ["su"])
+        tt(T.sd[:, 0, :], T.Sin[:, t, :], T.ds[:], OP.subtract, NC_, ["sarr", "Sin%d" % t, "su"], ["sd0"])
+        ts(T.wab[:], PH[:, 400:400 + NC_], 0.0, None, OP.is_lt, None, NC_, ["pW%d" % c for c in range(NCH)], ["wab"], [7])
+        tt(T.sd[:, 1, :], T.wab[:], T.sd[:, 0, :], OP.mult, NC_, ["wab", "sd0"], ["sd1"])
+        tt(T.OS[:, t, :], T.sd[:, 1, :], T.ds[:], OP.add, NC_, ["sd1", "su"], ["OS%d" % t])
+        sends["s", t] = send(nxt if t < RO - 1 else home, T.Sin[:, t + 1, :], T.OS[:, t, :], "rs%d" % (t + 1), ["OS%d" % t])
+        if t < RO - 1:
+            PA = PU[:, 160:160 + NCH * CC]
+            mm([(PA, T.Bk[:], T.wab[:], NCH * CC)], ["Bk", "wab"], ["pA"], [5])
+            op("V", lambda PA=PA: V.tensor_reduce(T.cn[:, 0:1], PA, AX.X, OP.add), vd(1), ["pA"], ["cn"], [5])
+            ts(T.cni[:, 0:1], T.cn[:, 0:1], -1.0, float(C), OP.mult, OP.add, 1, ["cn"], ["cni0"])
+            ts(T.cni[:, 1:2], T.cni[:, 0:1], 3, None, OP.bitwise_and, None, 1, ["cni0"], ["cni1"])
+            ts(T.tol[:, t + 1, 0:1], T.cni[:, 1:2], 2.0 - 256, None, OP.add, None, 1, ["cni1"], ["tol%da" % (t + 1)])
+
+    dma(T.yv[:], T.vs[:, 0:4096], 5.0, ["vs"], (), "out")
+    dma(T.yl[:], T.Lh[:], 2.0, (), (), "out", ext=[arrival(last, "rl%d_%d" % (RO, c)) for c in range(NCH)], after=[sends["l", RO - 1, c] for c in range(NCH)])
+    act(T.shb[:], T.Sin[:, RO, :], AF.Identity, 0.0, 1.0, NCH * CC, (), ["shb"], ext=[arrival(last, "rs%d" % RO)], after=[sends["s", RO - 1]])
+    mm([(ps[4][0:8, r:C:16], T.SI[:, 128 * r:128 * (r + 1):16], T.shb[:], NCH * CC) for r in range(16)], ["shb", "SI0", "SI1"], ["pM0"], [4], group=False)
+    act(T.yst[0:8, :], ps[4][0:8, 0:C], AF.Identity, 0.0, 1.0, C, ["pM0"], ["yst"], [4])
+    dma(T.ys[:], T.yst[0:8, :], 2.0, ["yst"], (), "out")
+    return ops
+
+
+def order(ops):
+    n = len(ops)
+    succ = [[] for _ in range(n)]; need = [0] * n
+    for i, o in enumerate(ops):
+        for j in o[3]: succ[j].append((i, 0.0 if o[0] == "P" and ops[j][0] == "P" else HOP))
+        for j in o[6]: succ[j].append((i, NET))
+        need[i] = len(o[3]) + len(o[6])
+    way = [0.0] * n
+    for i in range(n - 1, -1, -1):
+        way[i] = ops[i][2] + max([way[j] + d for j, d in succ[i]] + [0.0])
+    x = SEED
+    for i in range(n):
+        x = (x * 1103515245 + 12345) % 2147483648
+        way[i] += JIT * x / 2147483648
+    ready = [0.0] * n; free = {}; cand = {}
+    for i in range(n):
+        if need[i] == 0: cand.setdefault(ops[i][0], []).append(i)
+    seq = []; end = 0.0; bank = {}; extra = [[] for _ in range(n)]; fins = [0.0] * n
+
+    def when(i):
+        t = ready[i]
+        for b in ops[i][7]:
+            for qq, j in bank.get(b, {}).items():
+                if qq != ops[i][0]: t = max(t, fins[j] + HOP)
+        return t
+    while len(seq) < n:
+        best = None
+        for q, l in cand.items():
+            if not l: continue
+            t0 = max(free.get(q, 0.0), min(when(i) for i in l))
+            if best is None or t0 < best[0]: best = (t0, q)
+        t0, q = best
+        i = max((i for i in cand[q] if when(i) <= t0 + LOOK), key=lambda i: (way[i], -i))
+        cand[q].remove(i); st = max(t0, when(i)); fin = fins[i] = st + ops[i][2]
+        for b in ops[i][7]:
+            extra[i] += [j for qq, j in bank.get(b, {}).items() if qq != q]
+            bank.setdefault(b, {})[q] = i
+        free[q] = st + 0.1 if q == "S" else fin
+        seq.append(i); end = max(end, fin)
+        for j, d in succ[i]:
+            ready[j] = max(ready[j], fin + d); need[j] -= 1
+            if need[j] == 0: cand.setdefault(ops[j][0], []).append(j)
+    return seq, extra, end, fins
+
+
+PLAN = {}
+
+
+def rank_program(g, core, T, topo):
+    rank = T.rank_of(core)
+    if rank is None:
+        return
+    ops = build(g, T, topo, core, rank)
+    if "seq" not in PLAN:
+        PLAN["seq"], PLAN["extra"], PLAN["end"], PLAN["fins"] = order(ops)
+    Qs = {"V": g.vector, "A": g.scalar, "P": g.tensor, "G": g, "S": g.sync}
+    count = {}; done = {}; seen = {q: {} for q in Qs}
+
+    def wait(q, sem, val):
+        if seen[q].get(sem, 0) < val:
+            Qs[q].wait_ge(T.sem[sem], val); seen[q][sem] = val
+
+    for i in PLAN["seq"]:
+        q, calls, _, deps, sem, ext = ops[i][:6]
+        want = {}
+        for j in list(deps) + PLAN["extra"][i]:
+            if q == "P" and ops[j][0] == "P": continue
+            s, v = done[j]; want[s] = max(want.get(s, 0), v)
+        for s, v in ext: want[s] = v
+        for s, v in want.items(): wait(q, s, v)
+        for fn in calls:
+            ins = fn()
+            if sem is None:
+                s = "e" + q; ins.then_inc(T.sem[s], 1); count[s] = count.get(s, 0) + 1
+            elif sem[1] > 0:
+                s = sem[0]; ins.then_inc(T.sem[s], sem[1]); count[s] = count.get(s, 0) + sem[1]
+            else:
+                s = sem[0]; count[s] = count.get(s, 0) - sem[1]
+        done[i] = (s, count[s])
+    for s, v in count.items():
+        wait("G" if s == "sent" else "S", s, v)

@@ -1,3 +1,5 @@
+import math
+import numpy as np
 from concourse.mybir import AluOpType as OP, AxisListType as AX, ActivationFunctionType as AF
 
 NCH = 3
@@ -24,7 +26,7 @@ SCRATCH = {
     "shb": ("sbuf", [128, NCH * CC], "bfloat16"), "yst": ("sbuf", [128, C], "float32"),
     "a": ("sbuf", [128, C * K], "bfloat16"), "a16": ("sbuf", [128, C * K], "float16"), "Q": ("sbuf", [128, NRAW, 512], "bfloat16"),
     "F": ("sbuf", [128, NCH, 7 * NL], "bfloat16"), "D": ("sbuf", [128, NCH, 7 * NL], "float32"),
-    "R": ("sbuf", [128, NCH, 7 * NL], "bfloat16"), "E1": ("sbuf", [128, NCH, 7 * NL], "bfloat16"),
+    "R": ("sbuf", [128, NCH, 7 * NL], "float16"), "c7": ("sbuf", [128, G7], "bfloat16"), "E1": ("sbuf", [128, NCH, 7 * NL], "bfloat16"),
     "Vg": ("sbuf", [128, NCH, 7 * NL], "bfloat16"), "big": ("sbuf", [128, 512], "bfloat16"),
     "Xu": ("sbuf", [128, NCH, G7], "bfloat16"), "uf": ("sbuf", [128, NCH, G7], "float32"),
     "sf": ("sbuf", [128, NCH, G7], "float32"), "m8": ("sbuf", [128, G7], "bfloat16"), "Fs": ("sbuf", [128, NCH, NL], "bfloat16"),
@@ -52,9 +54,11 @@ SCRATCH = {
     "sd": ("sbuf", [128, 2, NCH * CC], "float32"), "pw": ("sbuf", [128, NCH, 16], "float32"), "vo": ("sbuf", [128, NCH, 16], "uint16"),
     "wab": ("sbuf", [128, NCH * CC], "bfloat16"),
     "cn": ("sbuf", [128, 8], "float32"), "cni": ("sbuf", [128, 8], "int32"), "tol": ("sbuf", [128, RO, 4], "float32"),
-    "one": ("sbuf", [128, 2048], "bfloat16"), "cI": ("sbuf", [128, 8, 128], "bfloat16"),
+    "one": ("sbuf", [128, 144], "bfloat16"), "cI": ("sbuf", [128, 11, 128], "bfloat16"),
+    "hx": ("sbuf", [128, NCH, NL], "float16"), "dgm": ("sbuf", [128, NL], "float32"), "bl2": ("sbuf", [128, 16], "uint16"),
+    "ea": ("sbuf", [128, 4, 64], "float32"),
     "Zs": ("sbuf", [128, 5, 144], "bfloat16"), "Z2": ("sbuf", [128, 144], "bfloat16"), "Z3": ("sbuf", [128, 144], "bfloat16"),
-    "SI": ("sbuf", [128, 16 * 128], "bfloat16"), "MP": ("sbuf", [128, 8, 128], "bfloat16"),
+    "SI": ("sbuf", [128, 128], "bfloat16"), "MP": ("sbuf", [128, 8, 128], "bfloat16"),
     "OPm": ("sbuf", [128, 6, 128], "bfloat16"), "PM": ("sbuf", [128, 7, 128], "bfloat16"), "Bk": ("sbuf", [128, 128], "bfloat16"),
     "ti": ("sbuf", [128, 4, 144], "int32"), "tf": ("sbuf", [128, 4, 144], "float32"),
     "pc": ("sbuf", [128, 8], "int32"), "pf": ("sbuf", [128, 16], "float32"),
@@ -69,11 +73,24 @@ SEMAPHORES = ["eV", "eA", "eP", "eG", "sent", "out"] + LOADS
 SEMAPHORES += ["rl%d_%d" % (t, c) for t in range(1, RO + 1) for c in range(NCH)]
 SEMAPHORES += ["rs%d" % t for t in range(1, RO + 1)]
 
+MS = [1, 5, 6, 7, 2, 3, 4]
+EQA = 0
+BIAS = {}
+TRIES = 1500
+ITER = 1
+MIX = 0.3
+QW = 0.5
+XB = [(0, 1), (1, 4), (4, 7)]
+YB = [(0, 4), (4, 7)]
+GP = 1
+RP = 2
+ED = 4
+FIX = 0.04
 G1V = ()
 SEED = 1
 JIT = 0.0
 RACT = 7
-CY, PCY, HOP, NET, LOOK, PIECE = 0.001, 0.0005, 0.12, 3.0, 0.05, 0.25
+CY, PCY, HOP, NET, LOOK, PIECE = 0.00087, 0.00044, 0.12, 3.0, 0.05, 0.22
 
 
 def coef(m, k):
@@ -101,7 +118,7 @@ def build(g, T, topo, core, rank):
         ops.append([q, calls if isinstance(calls, list) else [calls], dur, deps, sem, list(ext), list(after), list(b), (list(w) + [""])[0]])
         return i
 
-    def vd(nel, f=1.0): return 0.05 + max(64, nel * f) * CY
+    def vd(nel, f=1.0): return FIX + max(64, nel * f) * CY
     def ts(out, in0, s1, s2, o0, o1, nel, r, w, b=(), f=1.0, ext=(), after=()):
         if o1 is None: fn = lambda: V.tensor_scalar(out, in0, s1, None, o0)
         else: fn = lambda: V.tensor_scalar(out, in0, s1, s2, o0, o1)
@@ -113,7 +130,7 @@ def build(g, T, topo, core, rank):
     def ms(out, c, nel, w):
         return op("V", lambda: V.memset(out, c), vd(nel, 0.5), (), w)
     def act(out, in_, fn, bias, scale, nel, r, w, b=(), f=1.0, ext=(), after=()):
-        return op("A", lambda: A.activation(out, in_, fn, bias=bias, scale=scale), vd(nel, f) + 0.02, r, w, b, ext=ext, after=after)
+        return op("A", lambda: A.activation(out, in_, fn, bias=bias, scale=scale), vd(nel, f) + 0.06, r, w, b, ext=ext, after=after)
     def mm(lst, r, w, b, first=True, last=True, group=True):
         cut = 0; tot = 0
         for j, x in enumerate(lst):
@@ -151,7 +168,7 @@ def build(g, T, topo, core, rank):
     dma(T.xs[:], T.x[:], 5.0, (), ["xs"], "dx")
     dma(T.wti[:, 0:1], T.wt[:], 2.0, (), ["wti"], "dw")
     dma(T.s0i[0:8, :], T.s0[:], 2.0, (), ["s0i"], "ds")
-    dma(T.vs[:, 0:4096], T.v[:], 8.0, (), ["vs"], "dv")
+    dma(T.vs[:, 0:4096], T.v[:], 5.0, ["xs"], ["vs"], "dv")
 
     ms(T.one[:, 0:144], 1.0, 144, ["one"])
     sel_(T.cI[:, 1, :], T.one[:, 0:128], [[-1, 128]], OP.is_equal, 0, 1, 128, ["one"], ["I1"])
@@ -170,8 +187,11 @@ def build(g, T, topo, core, rank):
     for j, wgt in ((1, 2.0 ** 22), (2, 64.0)):
         ts(T.Zs[:, j, :], T.tf[:, 0, :], T.pf[:, 0:1], wgt, OP.is_equal, OP.mult, 144, ["tf0", "pf"], ["Z%d" % j])
     sel_(T.Z3[0:8, :], T.one[0:8, 0:144], [[1, 144]], OP.is_equal, -15, -16, 144, ["one"], ["Z3s"])
-    io(T.mpat[:], [[0, NCH], [4096, G7 // CC], [0, CC]], 4096 + 2 ** 19 + 2048, 0, NCH * G7, ["mp0"])
-    io(T.m8[:, 0:M7], [[8, 7], [0, CC]], 8, 0, M7, ["m8"], True)
+    for j0, j1, b0 in ((0, 1, 1), (1, 4, 5), (4, 7, 2)):
+        io(T.m8[:, j0 * CC:j1 * CC], [[8, j1 - j0], [0, CC]], 8 * b0, 0, 32, ["m8"], True)
+    ms(T.mpat[:], 0, NCH * G7, ["mp0"])
+    for c in range(NCH):
+        ts(T.mpat[:, c * G7:c * G7 + M7], T.m8[:, 0:M7], 512.0, float(2 ** 19 + 2048), OP.mult, OP.add, M7, ["m8", "mp0"], ["mp0"])
     nb = G7 // 16
     io(T.ti[:, 0, 0:nb], [[16, nb]], 0, 0, nb, ["b0"])
     ts(T.ti[:, 1, 0:nb], T.ti[:, 0, 0:nb], T.pf[:, 1:2], None, OP.add, None, nb, ["b0", "pf"], ["b1"])
@@ -186,10 +206,18 @@ def build(g, T, topo, core, rank):
     ms(T.P1[:], -1.0, NCH * G7, ["P1_%d" % c for c in range(NCH)])
     ms(T.ns[:], 0.0, 32, ["ns"])
     ms(T.K1[:], 0.0, NCH * 16, ["K1_%d" % c for c in range(NCH)])
-    ms(T.tol[:, 0, 0:1], 2.0 - 256, 1, ["tol0a"]); ms(T.big[:], 33024.0, 512, ["big"])
-    ms(T.one[:, 144:2048], 1.0, 1904, ["oneb"])
-    for hf in range(2):
-        sel_(T.SI[:, 1024 * hf:1024 * (hf + 1)], T.one[:, 0:1024], [[-1, 8], [-16, 8], [0, 16]], OP.is_equal, -8 * hf, 1, 1024, ["one", "oneb"], ["SI%d" % hf])
+    ms(T.tol[:, 0, 1:2], 2.5, 1, ["tol0b"])
+    ms(T.c7[:], -23.0 * 2 ** 22, G7, ["c7"])
+    if ED: ms(T.c7[:, 0:min(ED, 7) * CC], -7.0 * 2 ** 22, G7, ["c7"])
+    ms(T.big[:], 34816.0, 512, ["big"])
+    sel_(T.SI[:], T.one[:, 0:128], [[-1, 16], [-16, 8]], OP.is_equal, 0, 1, 128, ["one"], ["SI0"])
+    io(T.ti[:, 0, 64:64 + CC], [[1, CC]], 0, 0, CC, ["e0"])
+    cp(T.bl2[:, 0:CC], T.ti[:, 0, 64:64 + CC], CC, ["e0"], ["bl2"])
+    io(T.dgm[:], [[0, CC], [1, 16]], 0, 0, NL, ["dgm"], True)
+    ts(T.dgm[:], T.dgm[:], T.pf[:, 1:2], None, OP.is_equal, None, NL, ["dgm", "pf"], ["dgm"])
+    ms(T.ea[:], 1.0, 4 * 64, ["ea%d" % j for j in range(CC)])
+    for c in range(2, 5):
+        act(T.cI[:, 6 + c, :], T.cI[:, 1, :], AF.Identity, 0.0, float(-c), 128, ["I1"], ["In%d" % c])
     for rh in range(8):
         sel_(T.MP[:, rh, :], T.one[:, 0:128], [[-16, 8], [-1, 2], [0, 8]], OP.is_equal, -2 * rh, 1, 128, ["one"], ["MP%d" % rh])
     MPall = ["MP%d" % rh for rh in range(8)]
@@ -224,6 +252,7 @@ def build(g, T, topo, core, rank):
         tt(T.PM[:, m - 1, :], T.PM[:, m - 1, :], T.OPm[:, j, :], OP.subtract, 128, ["tm%d" % j, "PM%d" % m], ["PM%d" % m])
     PMall = ["PM%d" % m for m in range(1, 8)]
     io(T.ccp[:, 0:CC], [[1, CC]], 0, 0, CC, ["ccp"], True)
+    act(T.ccp[:, 0:CC], T.ccp[:, 0:CC], AF.Identity, 0.0, 1.0 / CC, CC, ["ccp"], ["ccp"])
     io(T.ti[:, 0, 32:32 + NCH * CC], [[16, NCH * CC]], 1025, 0, NCH * CC, ["d0"])
     ts(T.dm[:], T.ti[:, 0, 32:32 + NCH * CC], T.pf[:, 1:2], 2.0, OP.add, OP.mult, NCH * CC, ["d0", "pf"], ["dm"])
     for j in range(0, NOCOL, 1024):
@@ -254,7 +283,10 @@ def build(g, T, topo, core, rank):
         if onv:
             ts(Ta[:, a0:a0 + NL * K], T.xs[:].indirect(Lu), 1280.0, None, OP.add, None, NL * K, ["xs", "Lu%d_%d" % (t, c)], ["a" + s], f=1.56, ext=el, after=al)
         else:
-            act(Ta[:, a0:a0 + NL * K], T.xs[:].indirect(Lu), AF.Identity, 0.0, 1.0, NL * K, ["xs", "Lu%d_%d" % (t, c)], ["a" + s], f=1.56, ext=el, after=al)
+            w_ = PC // GP
+            for j in range(GP):
+                act(Ta[:, a0 + 16 * j * w_:a0 + 16 * (j + 1) * w_], T.xs[:].indirect(T.Lu[:, t, c * PC + j * w_:c * PC + (j + 1) * w_]), AF.Identity, 0.0, 1.0, 16 * w_,
+                    ["xs", "Lu%d_%d" % (t, c)], ["a%s_%d" % (s, j)], f=1.56, ext=el, after=al)
         ts(T.L16[:, c, :], Lu, -2048.0, None, OP.add, None, PC, ["Lu%d_%d" % (t, c)], ["L16" + s], f=0.5, ext=el, after=al)
         if c == 0:
             es = [arrival(prv, "rs%d" % t)] if t else []
@@ -263,15 +295,18 @@ def build(g, T, topo, core, rank):
             tt(T.pri[:], T.ns[:].indirect(T.bl[:, 0:NCH * nb]), T.mpat[:], OP.add, NCH * G7, ["ns", "bl", "mp0"], ["pri"], f=1.56)
             ts(T.prj[:], T.pri[:], 2 ** 19 + 7 * 4096 + 2048, None, OP.bitwise_and, None, NCH * G7, ["pri"], ["base"])
         Fall = []
-        for m0 in range(1, 8, MB):
-            mlist = list(range(m0, min(8, m0 + MB))); w_ = len(mlist) * NL
+        for j0, j1 in XB:
+            m0 = j0 + 1; mlist = MS[j0:j1]; w_ = len(mlist) * NL; on1 = j0 >= 4
             bk = rot[0] % NRAW; rot[0] += 1
             lst = [] if onv else [(ps[bk][:, 0:w_], T.cI[:, 1, :], T.big[:, 0:w_], w_)]
             for j, m in enumerate(mlist):
                 for k in range(K):
-                    if coef(m, k):
-                        lst.append((ps[bk][:, j * NL:(j + 1) * NL], T.cI[:, coef(m, k), :], Ta[:, a0 + k:a0 + NL * K:K], NL))
-            mm(lst, ["a" + s, "big"] + cIall, ["raw%d" % bk, "turn"], [bk])
+                    cf = coef(m, k) - (coef(1, k) if on1 else 0)
+                    if cf:
+                        lst.append((ps[bk][:, j * NL:(j + 1) * NL], T.cI[:, cf if cf > 0 else (0 if cf == -1 else 6 - cf), :], Ta[:, a0 + k:a0 + NL * K:K], NL))
+                if on1:
+                    lst.append((ps[bk][:, j * NL:(j + 1) * NL], T.cI[:, 1, :], T.F[:, c, 0:NL], NL))
+            mm(lst, ["a" + s, "big", "In2", "In3", "In4"] + ["a%s_%d" % (s, j) for j in range(GP)] + cIall + (Fall[:1] if on1 else []), ["raw%d" % bk, "turn%d" % bk], [bk])
             act(T.Q[:, bk, 0:w_], ps[bk][:, 0:w_], AF.Identity, -127.5, 1.0, w_, ["raw%d" % bk], ["Q%d" % bk], [bk])
             tt(T.F[:, c, (m0 - 1) * NL:(m0 - 1) * NL + w_], ps[bk][:, 0:w_], T.Q[:, bk, 0:w_], OP.subtract, w_, ["raw%d" % bk, "Q%d" % bk], ["F%s_%d" % (s, m0)], [bk], f=1)
             Fall.append("F%s_%d" % (s, m0))
@@ -292,19 +327,22 @@ def build(g, T, topo, core, rank):
     def phase_y(t, c, Fall):
         s = "%d" % c; W = 7 * NL
         Eall, Rall = [], []
-        for m0 in range(0, 7, MB):
-            m1 = min(7, m0 + MB); w_ = (m1 - m0) * NL; cs = slice(m0 * NL, m1 * NL); x = "%s_%d" % (s, m0)
+        for m0, m1 in YB:
+            w_ = (m1 - m0) * NL; cs = slice(m0 * NL, m1 * NL); x = "%s_%d" % (s, m0)
             bk = NRAW + rot[1] % 2; rot[1] += 1
             act(T.Vg[:, c, cs], T.vs[:, 0:4096].indirect(T.h16[:, c, m0 * CC:m1 * CC]), AF.Identity, 0.0, 1.0, w_, ["vs", "h16" + s], ["Vg" + x], f=1.56)
             mm([(ps[bk][:, 0:w_], T.cI[:, 0, :], T.F[:, c, cs], w_), (ps[bk][:, 0:w_], T.cI[:, 1, :], T.Vg[:, c, cs], w_)], ["Vg" + x] + Fall, ["raw%d" % bk], [bk])
             act(T.D[:, c, cs], ps[bk][:, 0:w_], AF.Abs, 0.0, 1.0, w_, ["raw%d" % bk], ["D" + x], [bk])
-            if m0 < RACT: act(T.R[:, c, cs], T.D[:, c, cs], AF.Identity, -256.0, 1.0, w_, ["D" + x], ["R" + x])
-            else: ts(T.R[:, c, cs], T.D[:, c, cs], -256.0, None, OP.add, None, w_, ["D" + x], ["R" + x])
-            ts(T.E1[:, c, cs], T.R[:, c, cs], T.tol[:, t, 0:1], -23.0 / 32, OP.is_le, OP.add, w_, ["R" + x, "tol%da" % t], ["E" + x], f=0.5)
-            Eall.append("E" + x); Rall.append("R" + x)
+            for m in range(m0, m1, RP):
+                c2 = slice(m * NL, min(m1, m + RP) * NL); n2 = c2.stop - c2.start
+                sel_(T.R[:, c, c2], T.D[:, c, c2], [[0, n2]], OP.is_gt, 1, 0, n2, ["D" + x], ["R%s_%d" % (s, m)])
+                Rall.append("R%s_%d" % (s, m))
+            if m0 >= ED: ts(T.E1[:, c, cs], T.D[:, c, cs], T.tol[:, t, 1:2], 2.0, OP.is_lt, OP.mult, w_, ["D" + x, "tol%db" % t], ["E" + x])
+            else: act(T.E1[:, c, cs], T.D[:, c, cs], AF.Sign, T.tol[:, t, 1:2], -1.0, w_, ["D" + x, "tol%db" % t], ["E" + x])
+            Eall.append("E" + x)
         def sums(out, B, j):
             return [(out, T.Zs[:, j, 15 - r:143 - r], B[:, c, r:W:16], M7) for r in range(16)]
-        mm(sums(PT[:, 0:M7], T.E1, 1), Eall + ["Z1"], ["pT"], [6])
+        mm([(PT[:, 0:M7], T.cI[:, 1, :], T.c7[:, 0:M7], M7)] + sums(PT[:, 0:M7], T.E1, 1), Eall + ["Z1", "c7"], ["pT"], [6])
         PF = PU[:, 256 + c * M7:256 + (c + 1) * M7]
         mm(sums(PF, T.R, 2) + [(PF, T.cI[:, 1, :], T.m8[:, 0:M7], M7)], Rall + ["Z2", "m8"], ["pfar" + s], [5])
         tt(T.Kk[:, c, CC:8 * CC], PT[:, 0:M7], T.P1[:, c, 0:M7], OP.max, M7, ["pT", "P1_" + s], ["Kk" + s], [6], f=1)
@@ -313,13 +351,19 @@ def build(g, T, topo, core, rank):
         tt(T.K1[:, c, 0:CC], T.K2[:, c, 0:CC], T.K2[:, c, CC:2 * CC], OP.min, CC, ["K2" + s], ["K1_" + s])
         Km = T.K1[:, c, 0:CC]
         ts(T.X[:, c, 0:CC], Km, 0.5, None, OP.add, None, CC, ["K1_" + s], ["X" + s])
-        tt(T.hn16[:, c, 0:CC], Km, T.X[:, c, 0:CC], OP.subtract, CC, ["K1_" + s, "X" + s], ["hn16" + s])
         tt(T.hn32[:, c, 0:CC], Km, T.X[:, c, 0:CC], OP.subtract, CC, ["K1_" + s, "X" + s], ["hn32" + s])
-        mm([(PH[:, r:NL:16], T.SI[:, 128 * r:128 * (r + 1)], T.hn16[:, c, 0:CC], CC) for r in range(16)], ["hn16" + s, "SI0", "SI1"], ["pH"], [7], group=False)
+        tt(T.hx[:, c, :], T.hn32[:, c, 0:CC].indirect(T.bl2[:, 0:CC]), T.dgm[:], OP.mult, NL, ["hn32" + s, "bl2", "dgm"], ["hx" + s], f=1.56)
+        mm([(PH[:, 0:NL], T.Bk[:], T.hx[:, c, :], NL)], ["hx" + s, "Bk"], ["pH"], [7])
+        J0 = CC - EQA; n0 = 16 * EQA
+        if EQA:
+            mm([(PT[:, 384:384 + n0], T.Bk[:], T.hx[:, c, 16 * J0:NL], n0)], ["hx" + s, "Bk"], ["pH2"], [6])
+            for j in range(J0, CC):
+                act(T.ea[:, j - J0, 0:NL - 16 * j], PT[:, 384 + 16 * (j - J0):384 + n0], AF.Abs, T.hn32[:, c, j:j + 1], -1.0, NL - 16 * j, ["pH2", "hn32" + s], ["ea%d" % j], [6])
+            act(T.eq[:, c * CC + J0:(c + 1) * CC, 0:n0], T.ea[:, 0:EQA, 0:n0], AF.Relu, 1.0, -1.0, EQA * n0, ["ea%d" % j for j in range(J0, CC)], ["eq%s_%d" % (s, j) for j in range(J0, CC)])
         ts(T.co[:, c, 0:CC], T.hn32[:, c, 0:CC], 2048.0, None, OP.add, None, CC, ["hn32" + s], ["co" + s])
         act(T.clm[:, c, :], T.cl[:].indirect(T.co[:, c, 0:CC]), AF.Relu, float(-t), 1.0, NL, ["cl", "clb", "co" + s], ["clm" + s], f=1.56)
         e0 = c * CC
-        for j in range(CC):
+        for j in range(J0):
             ts(T.eq[:, e0 + j, 0:NL - 16 * j], PH[:, 16 * j:NL], T.hn32[:, c, j:j + 1], None, OP.is_equal, None, NL - 16 * j, ["pH", "hn32" + s], ["eq%s_%d" % (s, j)], [7])
         PL = PH[:, 256:256 + PC]
         lst = []
@@ -337,7 +381,7 @@ def build(g, T, topo, core, rank):
             for m in range(m0, m1):
                 tt(T.Y[:, c * 7 + m, :], ps[bk][:, (m - m0) * PC:(m - m0 + 1) * PC], T.L16[:, c, :], OP.mult, PC, ["pM%d" % bi, "L16" + s], ["Y%s_%d" % (s, m)], [bk], f=1)
         PD = PT[:, 256:256 + PC]
-        mm([(PD, T.PM[:, m, :], T.Y[:, c * 7 + m, :], PC) for m in range(7)], PMall + ["Y%s_%d" % (s, m) for m in range(7)], ["pD"], [6])
+        mm([(PD, T.PM[:, MS[m] - 1, :], T.Y[:, c * 7 + m, :], PC) for m in range(7)], PMall + ["Y%s_%d" % (s, m) for m in range(7)], ["pD"], [6])
         tt(T.winP[:, c, :], PL, T.thr[:], OP.is_lt, PC, ["pL", "thr"], ["winP" + s], [7], f=1)
         tt(T.dw[:, c, :], PD, T.winP[:, c, :], OP.mult, PC, ["pD", "winP" + s], ["dw" + s], [6], f=1)
         tt(T.ln[:, c, :], T.dw[:, c, :], T.L16[:, c, :], OP.add, PC, ["dw" + s, "L16" + s], ["ln" + s])
@@ -348,10 +392,9 @@ def build(g, T, topo, core, rank):
         else:
             ts(T.Lf[:, cs], T.ln[:, c, :], 2048.0, None, OP.add, None, PC, ["ln" + s], ["Lf" + s])
             sends["l", t, c] = send(home, T.Lh[:, cs], T.Lf[:, cs], "rl%d_%d" % (t + 1, c), ["Lf" + s])
-        act(T.selc[:, c, 0:M7], T.sel[:, c, 0:M7], AF.Identity, 0.0, float(CC), M7, ["sel" + s], ["selc" + s])
         PP = PU[:, 128:128 + CC]
-        mm([(PP, T.cI[:, m, :], T.selc[:, c, (m - 1) * CC:m * CC], CC) for m in range(1, 8)] + [(PP, T.cI[:, 1, :], T.ccp[:, 0:CC], CC)], ["selc" + s, "ccp"], ["pP"], [5])
-        ts(T.fo[:, c, 0:CC], PP, 16.0, T.pf[:, 6:7], OP.mult, OP.add, CC, ["pP", "pf6"], ["fo" + s], [5])
+        mm([(PP, T.cI[:, m, :], T.sel[:, c, (m - 1) * CC:m * CC], CC) for m in range(1, 8)] + [(PP, T.cI[:, 1, :], T.ccp[:, 0:CC], CC)], ["sel" + s, "ccp"], ["pP"], [5])
+        ts(T.fo[:, c, 0:CC], PP, float(NL), T.pf[:, 6:7], OP.mult, OP.add, CC, ["pP", "pf6"], ["fo" + s], [5])
         act(T.Fs[:, c, :], T.F[:, c, :].indirect(T.fo[:, c, 0:CC]), AF.Identity, 0.0, 1.0, NL, ["fo" + s] + Fall, ["Fs" + s], f=1.56)
         PW = PH[:, 400 + c * CC:400 + (c + 1) * CC]
         mm([(PW, T.cI[:, 1, :], T.dm[:, c * CC:(c + 1) * CC], CC)] + [(PW, T.Z2[:, 15 - 2 * rh:143 - 2 * rh], T.winP[:, c, rh:PC:8], CC) for rh in range(8)], ["winP" + s, "Z2s", "dm"], ["pW" + s], [7])
@@ -382,12 +425,12 @@ def build(g, T, topo, core, rank):
             op("V", lambda PA=PA: V.tensor_reduce(T.cn[:, 0:1], PA, AX.X, OP.add), vd(1), ["pA"], ["cn"], [5])
             ts(T.cni[:, 0:1], T.cn[:, 0:1], -1.0, float(C), OP.mult, OP.add, 1, ["cn"], ["cni0"])
             ts(T.cni[:, 1:2], T.cni[:, 0:1], 3, None, OP.bitwise_and, None, 1, ["cni0"], ["cni1"])
-            ts(T.tol[:, t + 1, 0:1], T.cni[:, 1:2], 2.0 - 256, None, OP.add, None, 1, ["cni1"], ["tol%da" % (t + 1)])
+            ts(T.tol[:, t + 1, 1:2], T.cni[:, 1:2], 2.5, None, OP.add, None, 1, ["cni1"], ["tol%db" % (t + 1)])
 
     dma(T.yv[:], T.vs[:, 0:4096], 5.0, ["vs"], (), "out")
     dma(T.yl[:], T.Lh[:], 2.0, (), (), "out", ext=[arrival(last, "rl%d_%d" % (RO, c)) for c in range(NCH)], after=[sends["l", RO - 1, c] for c in range(NCH)])
     act(T.shb[:], T.Sin[:, RO, :], AF.Identity, 0.0, 1.0, NCH * CC, (), ["shb"], ext=[arrival(last, "rs%d" % RO)], after=[sends["s", RO - 1]])
-    mm([(ps[4][0:8, r:C:16], T.SI[:, 128 * r:128 * (r + 1):16], T.shb[:], NCH * CC) for r in range(16)], ["shb", "SI0", "SI1"], ["pM0"], [4], group=False)
+    mm([(ps[4][0:8, r:C:16], T.SI[:, 8 * r:8 * (r + 1)], T.shb[:], NCH * CC) for r in range(16)], ["shb", "SI0"], ["pM0"], [4], group=False)
     act(T.yst[0:8, :], ps[4][0:8, 0:C], AF.Identity, 0.0, 1.0, C, ["pM0"], ["yst"], [4])
     dma(T.ys[:], T.yst[0:8, :], 2.0, ["yst"], (), "out")
     return ops
@@ -406,7 +449,23 @@ def order(ops):
     x = SEED
     for i in range(n):
         x = (x * 1103515245 + 12345) % 2147483648
-        way[i] += JIT * x / 2147483648
+        way[i] += JIT * x / 2147483648 + BIAS.get(ops[i][8], 0.0)
+    best = None
+    for it in range(ITER):
+        res = place(ops, succ, list(need), way)
+        if best is None or res[2] < best[2]: best = res
+        w2 = [0.0] * n; nx = {}
+        for i in reversed(res[0]):
+            q = ops[i][0]
+            w2[i] = ops[i][2] + max([w2[j] + d for j, d in succ[i]] + [0.0])
+            if q in nx and q != "S": w2[i] = max(w2[i], w2[nx[q]] + ops[i][2] * QW)
+            nx[q] = i
+        way = [(1 - MIX) * a + MIX * b for a, b in zip(way, w2)]
+    return best
+
+
+def place(ops, succ, need, way):
+    n = len(ops)
     ready = [0.0] * n; free = {}; cand = {}
     for i in range(n):
         if need[i] == 0: cand.setdefault(ops[i][0], []).append(i)
@@ -438,6 +497,44 @@ def order(ops):
     return seq, extra, end, fins
 
 
+def replay(seq, extra, ops, dur, hop, net):
+    fin = [0.0] * len(ops); free = {}
+    for i in seq:
+        o = ops[i]; q = o[0]; t = free.get(q, 0.0)
+        for j in o[3]:
+            x = fin[j] + (0.0 if q == "P" and ops[j][0] == "P" else hop)
+            if x > t: t = x
+        for j in extra[i]:
+            if fin[j] + hop > t: t = fin[j] + hop
+        for j in o[6]:
+            if fin[j] + net > t: t = fin[j] + net
+        fin[i] = t + dur[i]; free[q] = t + 0.1 if q == "S" else fin[i]
+    return max(fin)
+
+
+def tuned(ops):
+    cases = [([o[2] * {"V": fv, "A": fa, "P": fp, "G": fv}.get(o[0], 1.0) + {"V": dv, "A": da}.get(o[0], 0.0) for o in ops], hop, net)
+             for fv, fa, fp, hop, net, dv, da in ((1, 1, 1, 0.1, 3.0, 0, 0), (1.4, 1.35, 1.3, 0.15, 4.0, 0, 0), (1, 1, 1, 0.06, 2.0, -0.03, 0.05),
+                                                  (1.15, 1.2, 1.3, 0.2, 3.0, -0.03, -0.04), (1, 1, 0.9, 0.06, 4.5, 0.02, 0))]
+    cnt = {}
+    for o in ops: cnt[o[8]] = cnt.get(o[8], 0) + 1
+    names = sorted(k for k, v in cnt.items() if k and v >= 4)
+    rnd = np.random.default_rng(SEED)
+    best = None
+    for it in range(TRIES + 1):
+        old = dict(BIAS)
+        for _ in range(int(rnd.choice((1, 2, 4))) if it else 0):
+            nm = names[int(rnd.integers(len(names)))]
+            BIAS[nm] = BIAS.get(nm, 0.0) + float(rnd.choice((-4, -2, -1, -0.5, 0.5, 1, 2, 4)))
+        res = order(ops)
+        v = [replay(res[0], res[1], ops, *cs) for cs in cases]
+        sc = sum(math.log(x) for x in v)
+        if best is None or sc <= best[0]: best = (sc, res, v)
+        else:
+            BIAS.clear(); BIAS.update(old)
+    return best
+
+
 PLAN = {}
 
 
@@ -447,7 +544,7 @@ def rank_program(g, core, T, topo):
         return
     ops = build(g, T, topo, core, rank)
     if "seq" not in PLAN:
-        PLAN["seq"], PLAN["extra"], PLAN["end"], PLAN["fins"] = order(ops)
+        PLAN["seq"], PLAN["extra"], PLAN["end"], PLAN["fins"] = tuned(ops)[1]
     Qs = {"V": g.vector, "A": g.scalar, "P": g.tensor, "G": g, "S": g.sync}
     count = {}; done = {}; seen = {q: {} for q in Qs}
 

import math
import numpy as np
from concourse.mybir import AluOpType as OP, AxisListType as AX, ActivationFunctionType as AF

NCH = 3
C, K, RO = 384, 8, 5
NL = C // NCH
CC = NL // 16
M7 = 7 * CC
G7 = (M7 + 15) // 16 * 16
PC = NL // 2
MB = 512 // NL
NRAW = 2
VW = 4096 + 2 * C + 16
NOCOL = 4096
NONE = float(2 ** 20 + NOCOL - 2048)

SCRATCH = {
    "xs": ("sbuf", [128, 4096], "bfloat16"), "vs": ("sbuf", [128, VW], "bfloat16"),
    "cl": ("sbuf", [128, VW], "bfloat16"),
    "lin": ("sbuf", [128, 192], "int32"), "wti": ("sbuf", [128, 4], "int32"), "s0i": ("sbuf", [128, C], "int32"),
    "s0b": ("sbuf", [128, C], "bfloat16"),
    "Lu": ("sbuf", [128, RO, 192], "uint16"), "Lo": ("sbuf", [128, RO, 192], "uint16"),
    "Lf": ("sbuf", [128, 192], "float32"), "Lh": ("sbuf", [128, 192], "float32"),
    "Sin": ("sbuf", [128, RO + 1, NCH * CC], "float32"), "OS": ("sbuf", [128, RO, NCH * CC], "float32"),
    "shb": ("sbuf", [128, NCH * CC], "bfloat16"), "yst": ("sbuf", [128, C], "float32"),
    "a": ("sbuf", [128, C * K], "bfloat16"), "a16": ("sbuf", [128, C * K], "float16"), "Q": ("sbuf", [128, NRAW, 512], "bfloat16"),
    "F": ("sbuf", [128, NCH, 7 * NL], "bfloat16"), "D": ("sbuf", [128, NCH, 7 * NL], "float32"),
    "R": ("sbuf", [128, NCH, 7 * NL], "float16"), "c7": ("sbuf", [128, G7], "bfloat16"), "E1": ("sbuf", [128, NCH, 7 * NL], "bfloat16"),
    "Vg": ("sbuf", [128, NCH, 7 * NL], "bfloat16"), "big": ("sbuf", [128, 512], "bfloat16"),
    "Xu": ("sbuf", [128, NCH, G7], "bfloat16"), "uf": ("sbuf", [128, NCH, G7], "float32"),
    "sf": ("sbuf", [128, NCH, G7], "float32"), "m8": ("sbuf", [128, G7], "bfloat16"), "Fs": ("sbuf", [128, NCH, NL], "bfloat16"),
    "eq": ("sbuf", [128, NCH * CC, NL], "bfloat16"), "clm": ("sbuf", [128, NCH, NL], "bfloat16"),
    "tag": ("sbuf", [128, RO, NL], "bfloat16"),
    "L16": ("sbuf", [128, NCH, PC], "float16"), "Y": ("sbuf", [128, NCH * 7, PC], "float16"),
    "winP": ("sbuf", [128, NCH, PC], "bfloat16"), "dl": ("sbuf", [128, NCH, PC], "float32"),
    "dw": ("sbuf", [128, NCH, PC], "float32"), "ln": ("sbuf", [128, NCH, PC], "float32"),
    "ns": ("sbuf", [128, 32], "float32"), "pri": ("sbuf", [128, NCH * G7], "int32"),
    "prj": ("sbuf", [128, NCH, G7], "int32"), "base": ("sbuf", [128, NCH, G7], "float32"),
    "ui": ("sbuf", [128, NCH, G7], "int32"), "u": ("sbuf", [128, NCH, G7], "int32"),
    "sq": ("sbuf", [128, NCH, G7], "int32"), "w37": ("sbuf", [128, NCH, G7], "int32"),
    "sh": ("sbuf", [128, NCH, G7], "int32"), "hs": ("sbuf", [128, NCH, G7], "int32"),
    "h": ("sbuf", [128, NCH, G7], "int32"), "h16": ("sbuf", [128, NCH, G7], "uint16"),
    "u7": ("sbuf", [128, NCH, G7], "int32"), "P1": ("sbuf", [128, NCH, G7], "float32"),
    "Kk": ("sbuf", [128, NCH, 8 * CC], "float32"), "K4": ("sbuf", [128, NCH, 4 * CC], "float32"),
    "K2": ("sbuf", [128, NCH, 2 * CC], "float32"), "K1": ("sbuf", [128, NCH, 16], "float32"),
    "Kb": ("sbuf", [128, NCH, 8 * CC], "float32"), "Kb4": ("sbuf", [128, NCH, 4 * CC], "float32"),
    "Kb2": ("sbuf", [128, NCH, 2 * CC], "float32"),
    "X": ("sbuf", [128, NCH, 16], "bfloat16"), "hn16": ("sbuf", [128, NCH, 16], "float16"),
    "hn32": ("sbuf", [128, NCH, 16], "float32"), "co": ("sbuf", [128, NCH, 16], "uint16"),
    "sel": ("sbuf", [128, NCH, G7], "bfloat16"), "selc": ("sbuf", [128, NCH, G7], "bfloat16"),
    "fo": ("sbuf", [128, NCH, 16], "uint16"), "k2i": ("sbuf", [128, NCH * CC], "int32"),
    "ds": ("sbuf", [128, NCH * CC], "int32"), "pre": ("sbuf", [128, NCH, 16], "float32"),
    "sd": ("sbuf", [128, 2, NCH * CC], "float32"), "pw": ("sbuf", [128, NCH, 16], "float32"), "vo": ("sbuf", [128, NCH, 16], "uint16"),
    "wab": ("sbuf", [128, NCH * CC], "bfloat16"),
    "cn": ("sbuf", [128, 8], "float32"), "cni": ("sbuf", [128, 8], "int32"), "tol": ("sbuf", [128, RO, 4], "float32"),
    "one": ("sbuf", [128, 144], "bfloat16"), "cI": ("sbuf", [128, 11, 128], "bfloat16"),
    "hx": ("sbuf", [128, NCH, NL], "float16"), "dgm": ("sbuf", [128, NL], "float32"), "bl2": ("sbuf", [128, 16], "uint16"),
    "ea": ("sbuf", [128, 4, 64], "float32"),
    "Zs": ("sbuf", [128, 5, 144], "bfloat16"), "Z2": ("sbuf", [128, 144], "bfloat16"), "Z3": ("sbuf", [128, 144], "bfloat16"),
    "SI": ("sbuf", [128, 128], "bfloat16"), "MP": ("sbuf", [128, 8, 128], "bfloat16"),
    "OPm": ("sbuf", [128, 6, 128], "bfloat16"), "PM": ("sbuf", [128, 7, 128], "bfloat16"), "Bk": ("sbuf", [128, 128], "bfloat16"),
    "ti": ("sbuf", [128, 4, 144], "int32"), "tf": ("sbuf", [128, 4, 144], "float32"),
    "pc": ("sbuf", [128, 8], "int32"), "pf": ("sbuf", [128, 16], "float32"),
    "thr": ("sbuf", [128, PC], "float32"), "mpat": ("sbuf", [128, NCH * G7], "int32"), "ccp": ("sbuf", [128, 16], "bfloat16"),
    "dm": ("sbuf", [128, NCH * CC], "float16"), "bl": ("sbuf", [128, 16], "uint16"),
}
for _b in range(8):
    SCRATCH["ps%d" % _b] = ("psum", [128, 512], "float32")

LOADS = ["dx", "dv", "dl", "dw", "ds"]
SEMAPHORES = ["eV", "eA", "eP", "eG", "sent", "out"] + LOADS
SEMAPHORES += ["rl%d_%d" % (t, c) for t in range(1, RO + 1) for c in range(NCH)]
SEMAPHORES += ["rs%d" % t for t in range(1, RO + 1)]

MS = [1, 5, 6, 7, 2, 3, 4]
EQA = 0
BIAS = {}
TRIES = 1500
ITER = 1
MIX = 0.3
QW = 0.5
XB = [(0, 1), (1, 4), (4, 7)]
YB = [(0, 4), (4, 7)]
GP = 1
RP = 2
ED = 4
FIX = 0.04
G1V = ()
SEED = 1
JIT = 0.0
RACT = 7
CY, PCY, HOP, NET, LOOK, PIECE = 0.00087, 0.00044, 0.12, 3.0, 0.05, 0.22


def coef(m, k):
    return m - k if k <= m else k


def build(g, T, topo, core, rank):
    n = len(T.cores)
    ops = []
    lastw, readers, bank = {}, {}, {}
    V, A, PE = g.vector, g.scalar, g.tensor

    def op(q, calls, dur, r=(), w=(), b=(), sem=None, ext=(), after=()):
        i = len(ops)
        deps = set()
        for x in r:
            if x in lastw: deps.add(lastw[x])
        for x in w:
            if x in lastw: deps.add(lastw[x])
            deps.update(readers.get(x, ()))
        for x in r: readers.setdefault(x, []).append(i)
        for x in w:
            lastw[x] = i; readers[x] = []
        deps.discard(i)
        ops.append([q, calls if isinstance(calls, list) else [calls], dur, deps, sem, list(ext), list(after), list(b), (list(w) + [""])[0]])
        return i

    def vd(nel, f=1.0): return FIX + max(64, nel * f) * CY
    def ts(out, in0, s1, s2, o0, o1, nel, r, w, b=(), f=1.0, ext=(), after=()):
        if o1 is None: fn = lambda: V.tensor_scalar(out, in0, s1, None, o0)
        else: fn = lambda: V.tensor_scalar(out, in0, s1, s2, o0, o1)
        return op("V", fn, vd(nel, f), r, w, b, ext=ext, after=after)
    def tt(out, in0, in1, o, nel, r, w, b=(), f=2.0, ext=(), after=()):
        return op("V", lambda: V.tensor_tensor(out, in0, in1, o), vd(nel, f), r, w, b, ext=ext, after=after)
    def cp(out, in_, nel, r, w, b=(), f=1.0):
        return op("V", lambda: V.tensor_copy(out, in_), vd(nel, f), r, w, b)
    def ms(out, c, nel, w):
        return op("V", lambda: V.memset(out, c), vd(nel, 0.5), (), w)
    def act(out, in_, fn, bias, scale, nel, r, w, b=(), f=1.0, ext=(), after=()):
        return op("A", lambda: A.activation(out, in_, fn, bias=bias, scale=scale), vd(nel, f) + 0.06, r, w, b, ext=ext, after=after)
    def mm(lst, r, w, b, first=True, last=True, group=True):
        cut = 0; tot = 0
        for j, x in enumerate(lst):
            tot += max(64, x[3]) * PCY
            if (b[0] < NRAW or not group) and tot > PIECE and j >= 1 and len(lst) - j >= 2:
                cut = j; break
        if cut:
            mm(lst[:cut], r, w, b, first, False, group)
            return mm(lst[cut:], r, w, b, False, last, group)
        calls = []; dur = 0.02
        for j, (o, l, x, nn) in enumerate(lst):
            st = (first and j == 0) if group else True
            sp = (last and j == len(lst) - 1) if group else True
            calls.append(lambda o=o, l=l, x=x, st=st, sp=sp: PE.matmul(o, l, x, st, sp))
            dur += max(64, nn) * PCY
        return op("P", calls, dur, r, w, b)
    def io(out, pat, base, cm, nel, w, small=False):
        if small: fn = lambda: g.iota(out, pat, base, cm, allow_small_or_imprecise_dtypes=True)
        else: fn = lambda: g.iota(out, pat, base, cm)
        return op("G", fn, 0.15 + 2 * nel * CY, (), w)
    def sel_(out, in_, pat, cmp, base, cm, nel, r, w):
        return op("G", lambda: g.affine_select(out, in_, pat, cmp, 0.0, base, cm), 0.2 + 2 * nel * CY, r, w)
    def dma(out, in_, dur, r, w, sem, ext=(), after=()):
        return op("S", lambda: g.sync.dma_start(out, in_), dur, r, w, sem=(sem, 16), ext=ext, after=after)
    def send(dst, out, in_, rs, r):
        rid, pid, _ = topo.addr(dst); mask = topo.mask(core, dst)
        ne = len(topo.engines(core, dst))
        return op("G", lambda: g.remote_dma(out, in_, T.sem[rs], T.sem.sent, pid, rid, mask), 0.6, r, (), sem=("sent", -ne))
    def arrival(src, rs):
        return (rs, len(topo.engines(src, core)))
    ps = [T["ps%d" % i] for i in range(8)]
    PU, PT, PH = ps[5], ps[6], ps[7]

    dma(T.lin[:], T.lanes[:], 2.0, (), ["lin"], "dl")
    dma(T.xs[:], T.x[:], 5.0, (), ["xs"], "dx")
    dma(T.wti[:, 0:1], T.wt[:], 2.0, (), ["wti"], "dw")
    dma(T.s0i[0:8, :], T.s0[:], 2.0, (), ["s0i"], "ds")
    dma(T.vs[:, 0:4096], T.v[:], 5.0, ["xs"], ["vs"], "dv")

    ms(T.one[:, 0:144], 1.0, 144, ["one"])
    sel_(T.cI[:, 1, :], T.one[:, 0:128], [[-1, 128]], OP.is_equal, 0, 1, 128, ["one"], ["I1"])
    for c in range(2, 8):
        act(T.cI[:, c, :], T.cI[:, 1, :], AF.Identity, 0.0, float(c), 128, ["I1"], ["I%d" % c])
    act(T.cI[:, 0, :], T.cI[:, 1, :], AF.Identity, 0.0, -1.0, 128, ["I1"], ["I0"])
    cIall = ["I%d" % c for c in range(8)]
    io(T.pc[:, 0:1], [[0, 1]], 0, 1, 1, ["pc0"])
    for j, (mk, nm) in enumerate(((112, "g16"), (15, "r"), (7, "k"), (8, "pb"))):
        ts(T.pc[:, 1 + j:2 + j], T.pc[:, 0:1], mk, None, OP.bitwise_and, None, 1, ["pc0"], ["pc" + nm])
    cp(T.pf[:, 0:4], T.pc[:, 1:5], 4, ["pcg16", "pcr", "pck", "pcpb"], ["pf"])
    cp(T.pf[:, 4:5], T.wti[:, 0:1], 1, ["wti"], ["wf"])
    ts(T.pf[:, 6:7], T.pf[:, 1:2], float(-NL), None, OP.add, None, 1, ["pf"], ["pf6"])
    io(T.tf[:, 0, :], [[1, 144]], -15, 0, 144, ["tf0"], True)
    ts(T.Zs[:, 0, :], T.tf[:, 0, :], T.pf[:, 0:1], T.pf[:, 4:5], OP.is_equal, OP.mult, 144, ["tf0", "pf", "wf"], ["ZW"])
    for j, wgt in ((1, 2.0 ** 22), (2, 64.0)):
        ts(T.Zs[:, j, :], T.tf[:, 0, :], T.pf[:, 0:1], wgt, OP.is_equal, OP.mult, 144, ["tf0", "pf"], ["Z%d" % j])
    sel_(T.Z3[0:8, :], T.one[0:8, 0:144], [[1, 144]], OP.is_equal, -15, -16, 144, ["one"], ["Z3s"])
    for j0, j1, b0 in ((0, 1, 1), (1, 4, 5), (4, 7, 2)):
        io(T.m8[:, j0 * CC:j1 * CC], [[8, j1 - j0], [0, CC]], 8 * b0, 0, 32, ["m8"], True)
    ms(T.mpat[:], 0, NCH * G7, ["mp0"])
    for c in range(NCH):
        ts(T.mpat[:, c * G7:c * G7 + M7], T.m8[:, 0:M7], 512.0, float(2 ** 19 + 2048), OP.mult, OP.add, M7, ["m8", "mp0"], ["mp0"])
    nb = G7 // 16
    io(T.ti[:, 0, 0:nb], [[16, nb]], 0, 0, nb, ["b0"])
    ts(T.ti[:, 1, 0:nb], T.ti[:, 0, 0:nb], T.pf[:, 1:2], None, OP.add, None, nb, ["b0", "pf"], ["b1"])
    ts(T.ti[:, 2, 0:nb], T.ti[:, 1, 0:nb], float(65536 // CC + 1), None, OP.mult, None, nb, ["b1"], ["b2"])
    ts(T.ti[:, 3, 0:nb], T.ti[:, 2, 0:nb], 16, None, OP.arith_shift_right, None, nb, ["b2"], ["b3"])
    ts(T.ti[:, 2, 0:nb], T.ti[:, 3, 0:nb], float(-CC), None, OP.mult, None, nb, ["b3"], ["b2"])
    tt(T.ti[:, 3, 0:nb], T.ti[:, 2, 0:nb], T.ti[:, 1, 0:nb], OP.add, nb, ["b2", "b1"], ["b3"])
    for c in range(NCH):
        ts(T.bl[:, c * nb:(c + 1) * nb], T.ti[:, 3, 0:nb], float(c * CC), None, OP.add, None, nb, ["b3", "bl"], ["bl"])
    ms(T.Kk[:], NONE, NCH * 8 * CC, ["Kk%d" % c for c in range(NCH)])
    ms(T.Kb[:], NONE, NCH * 8 * CC, ["Kb"])
    ms(T.P1[:], -1.0, NCH * G7, ["P1_%d" % c for c in range(NCH)])
    ms(T.ns[:], 0.0, 32, ["ns"])
    ms(T.K1[:], 0.0, NCH * 16, ["K1_%d" % c for c in range(NCH)])
    ms(T.tol[:, 0, 1:2], 2.5, 1, ["tol0b"])
    ms(T.c7[:], -23.0 * 2 ** 22, G7, ["c7"])
    if ED: ms(T.c7[:, 0:min(ED, 7) * CC], -7.0 * 2 ** 22, G7, ["c7"])
    ms(T.big[:], 34816.0, 512, ["big"])
    sel_(T.SI[:], T.one[:, 0:128], [[-1, 16], [-16, 8]], OP.is_equal, 0, 1, 128, ["one"], ["SI0"])
    io(T.ti[:, 0, 64:64 + CC], [[1, CC]], 0, 0, CC, ["e0"])
    cp(T.bl2[:, 0:CC], T.ti[:, 0, 64:64 + CC], CC, ["e0"], ["bl2"])
    io(T.dgm[:], [[0, CC], [1, 16]], 0, 0, NL, ["dgm"], True)
    ts(T.dgm[:], T.dgm[:], T.pf[:, 1:2], None, OP.is_equal, None, NL, ["dgm", "pf"], ["dgm"])
    ms(T.ea[:], 1.0, 4 * 64, ["ea%d" % j for j in range(CC)])
    for c in range(2, 5):
        act(T.cI[:, 6 + c, :], T.cI[:, 1, :], AF.Identity, 0.0, float(-c), 128, ["I1"], ["In%d" % c])
    for rh in range(8):
        sel_(T.MP[:, rh, :], T.one[:, 0:128], [[-16, 8], [-1, 2], [0, 8]], OP.is_equal, -2 * rh, 1, 128, ["one"], ["MP%d" % rh])
    MPall = ["MP%d" % rh for rh in range(8)]
    ms(T.tf[:, 1, 0:16], 0.5, 16, ["hf"]); ms(T.tf[:, 1, 16:32], 0.0, 16, ["zf"])
    op("V", lambda: V.tensor_tensor_scan(T.tf[:, 1, 32:48], T.tf[:, 1, 0:16], T.tf[:, 1, 16:32], 65536.0, OP.mult, OP.add), vd(16), ["hf", "zf"], ["pw2"])
    ts(T.tf[:, 1, 48:64], T.tf[:, 0, 15:31], T.pf[:, 1:2], None, OP.is_equal, None, 16, ["tf0", "pf"], ["dg"])
    tt(T.tf[:, 1, 64:80], T.tf[:, 1, 48:64], T.tf[:, 1, 32:48], OP.mult, 16, ["dg", "pw2"], ["dg2"])
    op("V", lambda: V.tensor_reduce(T.pf[:, 5:6], T.tf[:, 1, 64:80], AX.X, OP.add), vd(16), ["dg2"], ["pf5"])
    io(T.tf[:, 2, 0:128], [[16, 8], [0, 16]], 0, 0, 128, ["tf2"], True)
    ts(T.Bk[:], T.tf[:, 2, 0:128], T.pf[:, 0:1], None, OP.is_equal, None, 128, ["tf2", "pf"], ["Bk"])
    io(T.tf[:, 3, 0:128], [[16, 8], [8, 2], [0, 8]], 0, 0, 128, ["tf3"], True)
    ts(T.pf[:, 8:9], T.pf[:, 0:1], 8.0, None, OP.add, None, 1, ["pf"], ["pf8"])
    for p in range(2):
        col = T.pf[:, 0:1] if p == 0 else T.pf[:, 8:9]
        ts(T.OPm[:, p, :], T.tf[:, 3, 0:128], col, 65536.0, OP.is_equal, OP.mult, 128, ["tf3", "pf", "pf8"], ["OA%d" % p])
        ts(T.OPm[:, 2 + p, :], T.tf[:, 3, 0:128], col, T.pf[:, 5:6], OP.is_equal, OP.mult, 128, ["tf3", "pf", "pf8", "pf5"], ["OD%d" % p])
    ts(T.pf[:, 9:10], T.pf[:, 3:4], -1.0 / 16, 1.0, OP.mult, OP.add, 1, ["pf"], ["pf9"])
    for rh in range(8):
        ms(T.thr[:, rh:PC:8], 2.0 ** (16 - 2 * rh), CC, ["th%d" % rh])
    ts(T.thr[:], T.thr[:], T.pf[:, 9:10], -0.5, OP.mult, OP.add, PC, ["pf9"] + ["th%d" % rh for rh in range(8)], ["thr"])
    ts(T.pf[:, 10:11], T.pf[:, 3:4], 0.125, T.pf[:, 0:1], OP.mult, OP.add, 1, ["pf"], ["pf10"])
    ts(T.pf[:, 11:12], T.pf[:, 2:3], 1000.0, T.pf[:, 10:11], OP.mult, OP.add, 1, ["pf", "pf10"], ["pf11"])
    ts(T.Z2[:], T.tf[:, 0, :], T.pf[:, 11:12], -8192.0, OP.is_equal, OP.mult, 144, ["tf0", "pf11"], ["Z2s"])
    io(T.tf[:, 2, 0:128], [[64, 16], [1, 8]], 0, 0, 128, ["tf2"], True)
    ts(T.pf[:, 12:13], T.pf[:, 0:1], T.pf[:, 3:4], -8.0, OP.add, OP.mult, 1, ["pf"], ["pf12"])
    ts(T.pf[:, 13:14], T.pf[:, 12:13], T.pf[:, 2:3], None, OP.add, None, 1, ["pf", "pf12"], ["pf13"])
    ts(T.tf[:, 3, 0:128], T.tf[:, 2, 0:128], T.pf[:, 13:14], None, OP.add, None, 128, ["tf2", "pf13"], ["tf3"])
    for m in range(1, 8):
        j = 4 + (m & 1)
        sel_(T.OPm[:, j, :], T.cI[:, 1, :], [[0, 16], [-1, 8]], OP.is_ge, m, 0, 128, ["I1"], ["tm%d" % j])
        ts(T.PM[:, m - 1, :], T.tf[:, 3, 0:128], float(m), None, OP.is_equal, None, 128, ["tf3"], ["PM%d" % m])
        tt(T.PM[:, m - 1, :], T.PM[:, m - 1, :], T.OPm[:, j, :], OP.subtract, 128, ["tm%d" % j, "PM%d" % m], ["PM%d" % m])
    PMall = ["PM%d" % m for m in range(1, 8)]
    io(T.ccp[:, 0:CC], [[1, CC]], 0, 0, CC, ["ccp"], True)
    act(T.ccp[:, 0:CC], T.ccp[:, 0:CC], AF.Identity, 0.0, 1.0 / CC, CC, ["ccp"], ["ccp"])
    io(T.ti[:, 0, 32:32 + NCH * CC], [[16, NCH * CC]], 1025, 0, NCH * CC, ["d0"])
    ts(T.dm[:], T.ti[:, 0, 32:32 + NCH * CC], T.pf[:, 1:2], 2.0, OP.add, OP.mult, NCH * CC, ["d0", "pf"], ["dm"])
    for j in range(0, NOCOL, 1024):
        ms(T.cl[:, j:j + 1024], 0.0, 1024, ["cl"])
    ms(T.cl[:, NOCOL:VW], 64.0, VW - NOCOL, ["cl"])
    ms(T.vs[:, 4096:VW], 0.0, VW - 4096, ["vsb"])
    for t in range(RO):
        ms(T.tag[:, t, :], float(t + 1), NL, ["tag%d" % t])
    for c in range(NCH):
        cp(T.Lu[:, 0, c * PC:(c + 1) * PC], T.lin[:, c * PC:(c + 1) * PC], PC, ["lin"], ["Lu0_%d" % c])
    cp(T.s0b[0:8, :], T.s0i[0:8, :], C, ["s0i"], ["s0b"])
    mm([(PU[:, 200:200 + NCH * CC], T.Z3[0:8, 15 - r:143 - r], T.s0b[0:8, r:C:16], NCH * CC) for r in range(16)], ["Z3s", "s0b"], ["pS"], [5])
    act(T.Sin[:, 0, :], PU[:, 200:200 + NCH * CC], AF.Identity, 0.0, 1.0, NCH * CC, ["pS"], ["Sin0"], [5])

    nxt = T.cores[(rank + 1) % n]; prv = T.cores[(rank - 1) % n]
    home = T.cores[(rank - (RO - 1)) % n]; last = T.cores[(rank + RO - 1) % n]
    sends = {}
    rot = [0, 0]

    def phase_x(t, c):
        s = "%d" % c
        Lu = T.Lu[:, t, c * PC:(c + 1) * PC]
        el = [arrival(prv, "rl%d_%d" % (t, c))] if t else []
        al = [sends["l", t - 1, c]] if t else []
        a0 = c * NL * K
        onv = c in G1V
        Ta = T.a16 if onv else T.a
        if onv:
            ts(Ta[:, a0:a0 + NL * K], T.xs[:].indirect(Lu), 1280.0, None, OP.add, None, NL * K, ["xs", "Lu%d_%d" % (t, c)], ["a" + s], f=1.56, ext=el, after=al)
        else:
            w_ = PC // GP
            for j in range(GP):
                act(Ta[:, a0 + 16 * j * w_:a0 + 16 * (j + 1) * w_], T.xs[:].indirect(T.Lu[:, t, c * PC + j * w_:c * PC + (j + 1) * w_]), AF.Identity, 0.0, 1.0, 16 * w_,
                    ["xs", "Lu%d_%d" % (t, c)], ["a%s_%d" % (s, j)], f=1.56, ext=el, after=al)
        ts(T.L16[:, c, :], Lu, -2048.0, None, OP.add, None, PC, ["Lu%d_%d" % (t, c)], ["L16" + s], f=0.5, ext=el, after=al)
        if c == 0:
            es = [arrival(prv, "rs%d" % t)] if t else []
            as_ = [sends["s", t - 1]] if t else []
            act(T.ns[:, 0:NCH * CC], T.Sin[:, t, :], AF.Identity, 32768.0, -4096.0, NCH * CC, ["Sin%d" % t], ["ns", "sarr"], ext=es, after=as_)
            tt(T.pri[:], T.ns[:].indirect(T.bl[:, 0:NCH * nb]), T.mpat[:], OP.add, NCH * G7, ["ns", "bl", "mp0"], ["pri"], f=1.56)
            ts(T.prj[:], T.pri[:], 2 ** 19 + 7 * 4096 + 2048, None, OP.bitwise_and, None, NCH * G7, ["pri"], ["base"])
        Fall = []
        for j0, j1 in XB:
            m0 = j0 + 1; mlist = MS[j0:j1]; w_ = len(mlist) * NL; on1 = j0 >= 4
            bk = rot[0] % NRAW; rot[0] += 1
            lst = [] if onv else [(ps[bk][:, 0:w_], T.cI[:, 1, :], T.big[:, 0:w_], w_)]
            for j, m in enumerate(mlist):
                for k in range(K):
                    cf = coef(m, k) - (coef(1, k) if on1 else 0)
                    if cf:
                        lst.append((ps[bk][:, j * NL:(j + 1) * NL], T.cI[:, cf if cf > 0 else (0 if cf == -1 else 6 - cf), :], Ta[:, a0 + k:a0 + NL * K:K], NL))
                if on1:
                    lst.append((ps[bk][:, j * NL:(j + 1) * NL], T.cI[:, 1, :], T.F[:, c, 0:NL], NL))
            mm(lst, ["a" + s, "big", "In2", "In3", "In4"] + ["a%s_%d" % (s, j) for j in range(GP)] + cIall + (Fall[:1] if on1 else []), ["raw%d" % bk, "turn%d" % bk], [bk])
            act(T.Q[:, bk, 0:w_], ps[bk][:, 0:w_], AF.Identity, -127.5, 1.0, w_, ["raw%d" % bk], ["Q%d" % bk], [bk])
            tt(T.F[:, c, (m0 - 1) * NL:(m0 - 1) * NL + w_], ps[bk][:, 0:w_], T.Q[:, bk, 0:w_], OP.subtract, w_, ["raw%d" % bk, "Q%d" % bk], ["F%s_%d" % (s, m0)], [bk], f=1)
            Fall.append("F%s_%d" % (s, m0))
        mm([(PU[:, 0:M7], T.Zs[:, 0, 15 - r:143 - r], T.F[:, c, r:7 * NL:16], M7) for r in range(16)], Fall + ["ZW"], ["pu"], [5])
        S7 = slice(0, M7); C0 = 2 ** 19 + 4096
        act(T.Xu[:, c, S7], PU[:, 0:M7], AF.Identity, C0 - 2047.5, 1.0, M7, ["pu"], ["Xu" + s], [5])
        tt(T.uf[:, c, S7], PU[:, 0:M7], T.Xu[:, c, S7], OP.subtract, M7, ["pu", "Xu" + s], ["uf" + s], [5], f=1)
        act(T.sf[:, c, S7], T.uf[:, c, S7], AF.Square, C0 + 592.0, 1.0, M7, ["uf" + s], ["sf" + s])
        ts(T.sq[:, c, S7], T.sf[:, c, S7], -592.0 * 592, None, OP.add, None, M7, ["sf" + s], ["sq" + s])
        ts(T.h[:, c, S7], T.sq[:, c, S7], 5, 4095, OP.arith_shift_right, OP.bitwise_and, M7, ["sq" + s], ["h" + s])
        cp(T.h16[:, c, S7], T.h[:, c, S7], M7, ["h" + s], ["h16" + s])
        tt(T.P1[:, c, S7], T.prj[:, c, S7], T.h[:, c, S7], OP.add, M7, ["base", "h" + s], ["P1_" + s])
        if c == NCH - 1:
            cp(T.ui[:, :, S7], T.uf[:, :, S7], NCH * M7, ["uf%d" % j for j in range(NCH)], ["ui"])
            ts(T.u7[:, :, S7], T.ui[:, :, S7], 7, None, OP.bitwise_and, None, NCH * M7, ["ui"], ["u7"])
        return Fall

    def phase_y(t, c, Fall):
        s = "%d" % c; W = 7 * NL
        Eall, Rall = [], []
        for m0, m1 in YB:
            w_ = (m1 - m0) * NL; cs = slice(m0 * NL, m1 * NL); x = "%s_%d" % (s, m0)
            bk = NRAW + rot[1] % 2; rot[1] += 1
            act(T.Vg[:, c, cs], T.vs[:, 0:4096].indirect(T.h16[:, c, m0 * CC:m1 * CC]), AF.Identity, 0.0, 1.0, w_, ["vs", "h16" + s], ["Vg" + x], f=1.56)
            mm([(ps[bk][:, 0:w_], T.cI[:, 0, :], T.F[:, c, cs], w_), (ps[bk][:, 0:w_], T.cI[:, 1, :], T.Vg[:, c, cs], w_)], ["Vg" + x] + Fall, ["raw%d" % bk], [bk])
            act(T.D[:, c, cs], ps[bk][:, 0:w_], AF.Abs, 0.0, 1.0, w_, ["raw%d" % bk], ["D" + x], [bk])
            for m in range(m0, m1, RP):
                c2 = slice(m * NL, min(m1, m + RP) * NL); n2 = c2.stop - c2.start
                sel_(T.R[:, c, c2], T.D[:, c, c2], [[0, n2]], OP.is_gt, 1, 0, n2, ["D" + x], ["R%s_%d" % (s, m)])
                Rall.append("R%s_%d" % (s, m))
            if m0 >= ED: ts(T.E1[:, c, cs], T.D[:, c, cs], T.tol[:, t, 1:2], 2.0, OP.is_lt, OP.mult, w_, ["D" + x, "tol%db" % t], ["E" + x])
            else: act(T.E1[:, c, cs], T.D[:, c, cs], AF.Sign, T.tol[:, t, 1:2], -1.0, w_, ["D" + x, "tol%db" % t], ["E" + x])
            Eall.append("E" + x)
        def sums(out, B, j):
            return [(out, T.Zs[:, j, 15 - r:143 - r], B[:, c, r:W:16], M7) for r in range(16)]
        mm([(PT[:, 0:M7], T.cI[:, 1, :], T.c7[:, 0:M7], M7)] + sums(PT[:, 0:M7], T.E1, 1), Eall + ["Z1", "c7"], ["pT"], [6])
        PF = PU[:, 256 + c * M7:256 + (c + 1) * M7]
        mm(sums(PF, T.R, 2) + [(PF, T.cI[:, 1, :], T.m8[:, 0:M7], M7)], Rall + ["Z2", "m8"], ["pfar" + s], [5])
        tt(T.Kk[:, c, CC:8 * CC], PT[:, 0:M7], T.P1[:, c, 0:M7], OP.max, M7, ["pT", "P1_" + s], ["Kk" + s], [6], f=1)
        tt(T.K4[:, c, :], T.Kk[:, c, 0:4 * CC], T.Kk[:, c, 4 * CC:8 * CC], OP.min, 4 * CC, ["Kk" + s], ["K4" + s])
        tt(T.K2[:, c, :], T.K4[:, c, 0:2 * CC], T.K4[:, c, 2 * CC:4 * CC], OP.min, 2 * CC, ["K4" + s], ["K2" + s])
        tt(T.K1[:, c, 0:CC], T.K2[:, c, 0:CC], T.K2[:, c, CC:2 * CC], OP.min, CC, ["K2" + s], ["K1_" + s])
        Km = T.K1[:, c, 0:CC]
        ts(T.X[:, c, 0:CC], Km, 0.5, None, OP.add, None, CC, ["K1_" + s], ["X" + s])
        tt(T.hn32[:, c, 0:CC], Km, T.X[:, c, 0:CC], OP.subtract, CC, ["K1_" + s, "X" + s], ["hn32" + s])
        tt(T.hx[:, c, :], T.hn32[:, c, 0:CC].indirect(T.bl2[:, 0:CC]), T.dgm[:], OP.mult, NL, ["hn32" + s, "bl2", "dgm"], ["hx" + s], f=1.56)
        mm([(PH[:, 0:NL], T.Bk[:], T.hx[:, c, :], NL)], ["hx" + s, "Bk"], ["pH"], [7])
        J0 = CC - EQA; n0 = 16 * EQA
        if EQA:
            mm([(PT[:, 384:384 + n0], T.Bk[:], T.hx[:, c, 16 * J0:NL], n0)], ["hx" + s, "Bk"], ["pH2"], [6])
            for j in range(J0, CC):
                act(T.ea[:, j - J0, 0:NL - 16 * j], PT[:, 384 + 16 * (j - J0):384 + n0], AF.Abs, T.hn32[:, c, j:j + 1], -1.0, NL - 16 * j, ["pH2", "hn32" + s], ["ea%d" % j], [6])
            act(T.eq[:, c * CC + J0:(c + 1) * CC, 0:n0], T.ea[:, 0:EQA, 0:n0], AF.Relu, 1.0, -1.0, EQA * n0, ["ea%d" % j for j in range(J0, CC)], ["eq%s_%d" % (s, j) for j in range(J0, CC)])
        ts(T.co[:, c, 0:CC], T.hn32[:, c, 0:CC], 2048.0, None, OP.add, None, CC, ["hn32" + s], ["co" + s])
        act(T.clm[:, c, :], T.cl[:].indirect(T.co[:, c, 0:CC]), AF.Relu, float(-t), 1.0, NL, ["cl", "clb", "co" + s], ["clm" + s], f=1.56)
        e0 = c * CC
        for j in range(J0):
            ts(T.eq[:, e0 + j, 0:NL - 16 * j], PH[:, 16 * j:NL], T.hn32[:, c, j:j + 1], None, OP.is_equal, None, NL - 16 * j, ["pH", "hn32" + s], ["eq%s_%d" % (s, j)], [7])
        PL = PH[:, 256:256 + PC]
        lst = []
        for p in range(2):
            lst.append((PL, T.OPm[:, p, :], T.clm[:, c, p:NL:2], PC))
            lst.append((PL, T.OPm[:, 2 + p, :], T.eq[:, e0:e0 + CC, p:16:2], PC))
            for j in range(CC - 1):
                lst.append((PH[:, 256 + 8 * (j + 1):256 + PC], T.OPm[:, p, :], T.eq[:, e0 + j, 16 + p:NL - 16 * j:2], PC - 8 * (j + 1)))
        mm(lst, ["clm" + s, "OA0", "OA1", "OD0", "OD1"] + ["eq%s_%d" % (s, j) for j in range(CC)], ["pL"], [7])
        tt(T.sel[:, c, :], T.K1[:, c, :].indirect(T.bl[:, 0:nb]), T.P1[:, c, :], OP.is_equal, G7, ["K1_" + s, "bl", "P1_" + s], ["sel" + s], f=1.56)
        mper = 512 // PC
        for bi, m0 in enumerate(range(0, 7, mper if 7 * PC <= 512 else 4)):
            m1 = min(7, m0 + (mper if 7 * PC <= 512 else 4)); bk = 4; bi = 0
            mm([(ps[bk][:, rh:(m1 - m0) * PC:8], T.MP[:, rh, :], T.sel[:, c, m0 * CC:m1 * CC], (m1 - m0) * CC) for rh in range(8)], ["sel" + s] + MPall, ["pM%d" % bi], [bk], group=False)
            for m in range(m0, m1):
                tt(T.Y[:, c * 7 + m, :], ps[bk][:, (m - m0) * PC:(m - m0 + 1) * PC], T.L16[:, c, :], OP.mult, PC, ["pM%d" % bi, "L16" + s], ["Y%s_%d" % (s, m)], [bk], f=1)
        PD = PT[:, 256:256 + PC]
        mm([(PD, T.PM[:, MS[m] - 1, :], T.Y[:, c * 7 + m, :], PC) for m in range(7)], PMall + ["Y%s_%d" % (s, m) for m in range(7)], ["pD"], [6])
        tt(T.winP[:, c, :], PL, T.thr[:], OP.is_lt, PC, ["pL", "thr"], ["winP" + s], [7], f=1)
        tt(T.dw[:, c, :], PD, T.winP[:, c, :], OP.mult, PC, ["pD", "winP" + s], ["dw" + s], [6], f=1)
        tt(T.ln[:, c, :], T.dw[:, c, :], T.L16[:, c, :], OP.add, PC, ["dw" + s, "L16" + s], ["ln" + s])
        cs = slice(c * PC, (c + 1) * PC)
        if t < RO - 1:
            ts(T.Lo[:, t, cs], T.ln[:, c, :], 2048.0, None, OP.add, None, PC, ["ln" + s], ["Lo%d_%d" % (t, c)])
            sends["l", t, c] = send(nxt, T.Lu[:, t + 1, cs], T.Lo[:, t, cs], "rl%d_%d" % (t + 1, c), ["Lo%d_%d" % (t, c)])
        else:
            ts(T.Lf[:, cs], T.ln[:, c, :], 2048.0, None, OP.add, None, PC, ["ln" + s], ["Lf" + s])
            sends["l", t, c] = send(home, T.Lh[:, cs], T.Lf[:, cs], "rl%d_%d" % (t + 1, c), ["Lf" + s])
        PP = PU[:, 128:128 + CC]
        mm([(PP, T.cI[:, m, :], T.sel[:, c, (m - 1) * CC:m * CC], CC) for m in range(1, 8)] + [(PP, T.cI[:, 1, :], T.ccp[:, 0:CC], CC)], ["sel" + s, "ccp"], ["pP"], [5])
        ts(T.fo[:, c, 0:CC], PP, float(NL), T.pf[:, 6:7], OP.mult, OP.add, CC, ["pP", "pf6"], ["fo" + s], [5])
        act(T.Fs[:, c, :], T.F[:, c, :].indirect(T.fo[:, c, 0:CC]), AF.Identity, 0.0, 1.0, NL, ["fo" + s] + Fall, ["Fs" + s], f=1.56)
        PW = PH[:, 400 + c * CC:400 + (c + 1) * CC]
        mm([(PW, T.cI[:, 1, :], T.dm[:, c * CC:(c + 1) * CC], CC)] + [(PW, T.Z2[:, 15 - 2 * rh:143 - 2 * rh], T.winP[:, c, rh:PC:8], CC) for rh in range(8)], ["winP" + s, "Z2s", "dm"], ["pW" + s], [7])
        tt(T.pw[:, c, 0:CC], PW, T.hn32[:, c, 0:CC], OP.max, CC, ["pW" + s, "hn32" + s], ["pw" + s], [7], f=1)
        ts(T.vo[:, c, 0:CC], T.pw[:, c, 0:CC], 2048.0, None, OP.add, None, CC, ["pw" + s], ["vo" + s])
        if c < NCH - 1:
            cp(T.cl[:, 0:VW].indirect(T.vo[:, c, 0:CC]), T.tag[:, t, :], NL, ["vo" + s, "tag%d" % t], ["cl"], f=3.8)

    NC_ = NCH * CC
    for t in range(RO):
        Fs_ = [phase_x(t, c) for c in range(NCH)]
        for c in range(NCH): phase_y(t, c, Fs_[c])
        for c in range(NCH):
            cp(T.vs[:].indirect(T.vo[:, c, 0:CC]), T.Fs[:, c, :], NL, ["vo%d" % c, "Fs%d" % c, "vsb"], ["vs"], f=3.8)
        tt(T.Kb[:, :, CC:8 * CC], PU[:, 256:256 + NCH * M7], T.u7[:, :, 0:M7], OP.add, NCH * M7, ["pfar%d" % c for c in range(NCH)] + ["u7"], ["Kb"], [5], f=1)
        tt(T.Kb4[:], T.Kb[:, :, 0:4 * CC], T.Kb[:, :, 4 * CC:8 * CC], OP.min, 4 * NC_, ["Kb"], ["Kb4"])
        tt(T.Kb2[:], T.Kb4[:, :, 0:2 * CC], T.Kb4[:, :, 2 * CC:4 * CC], OP.min, 2 * NC_, ["Kb4"], ["Kb2"])
        tt(T.k2i[:], T.Kb2[:, :, 0:CC], T.Kb2[:, :, CC:2 * CC], OP.min, NC_, ["Kb2"], ["k2i"])
        ts(T.ds[:], T.k2i[:], 7, None, OP.bitwise_and, None, NC_, ["k2i"], ["su"])
        tt(T.sd[:, 0, :], T.Sin[:, t, :], T.ds[:], OP.subtract, NC_, ["sarr", "Sin%d" % t, "su"], ["sd0"])
        ts(T.wab[:], PH[:, 400:400 + NC_], 0.0, None, OP.is_lt, None, NC_, ["pW%d" % c for c in range(NCH)], ["wab"], [7])
        tt(T.sd[:, 1, :], T.wab[:], T.sd[:, 0, :], OP.mult, NC_, ["wab", "sd0"], ["sd1"])
        tt(T.OS[:, t, :], T.sd[:, 1, :], T.ds[:], OP.add, NC_, ["sd1", "su"], ["OS%d" % t])
        sends["s", t] = send(nxt if t < RO - 1 else home, T.Sin[:, t + 1, :], T.OS[:, t, :], "rs%d" % (t + 1), ["OS%d" % t])
        if t < RO - 1:
            PA = PU[:, 160:160 + NCH * CC]
            mm([(PA, T.Bk[:], T.wab[:], NCH * CC)], ["Bk", "wab"], ["pA"], [5])
            op("V", lambda PA=PA: V.tensor_reduce(T.cn[:, 0:1], PA, AX.X, OP.add), vd(1), ["pA"], ["cn"], [5])
            ts(T.cni[:, 0:1], T.cn[:, 0:1], -1.0, float(C), OP.mult, OP.add, 1, ["cn"], ["cni0"])
            ts(T.cni[:, 1:2], T.cni[:, 0:1], 3, None, OP.bitwise_and, None, 1, ["cni0"], ["cni1"])
            ts(T.tol[:, t + 1, 1:2], T.cni[:, 1:2], 2.5, None, OP.add, None, 1, ["cni1"], ["tol%db" % (t + 1)])

    dma(T.yv[:], T.vs[:, 0:4096], 5.0, ["vs"], (), "out")
    dma(T.yl[:], T.Lh[:], 2.0, (), (), "out", ext=[arrival(last, "rl%d_%d" % (RO, c)) for c in range(NCH)], after=[sends["l", RO - 1, c] for c in range(NCH)])
    act(T.shb[:], T.Sin[:, RO, :], AF.Identity, 0.0, 1.0, NCH * CC, (), ["shb"], ext=[arrival(last, "rs%d" % RO)], after=[sends["s", RO - 1]])
    mm([(ps[4][0:8, r:C:16], T.SI[:, 8 * r:8 * (r + 1)], T.shb[:], NCH * CC) for r in range(16)], ["shb", "SI0"], ["pM0"], [4], group=False)
    act(T.yst[0:8, :], ps[4][0:8, 0:C], AF.Identity, 0.0, 1.0, C, ["pM0"], ["yst"], [4])
    dma(T.ys[:], T.yst[0:8, :], 2.0, ["yst"], (), "out")
    return ops


def order(ops):
    n = len(ops)
    succ = [[] for _ in range(n)]; need = [0] * n
    for i, o in enumerate(ops):
        for j in o[3]: succ[j].append((i, 0.0 if o[0] == "P" and ops[j][0] == "P" else HOP))
        for j in o[6]: succ[j].append((i, NET))
        need[i] = len(o[3]) + len(o[6])
    way = [0.0] * n
    for i in range(n - 1, -1, -1):
        way[i] = ops[i][2] + max([way[j] + d for j, d in succ[i]] + [0.0])
    x = SEED
    for i in range(n):
        x = (x * 1103515245 + 12345) % 2147483648
        way[i] += JIT * x / 2147483648 + BIAS.get(ops[i][8], 0.0)
    best = None
    for it in range(ITER):
        res = place(ops, succ, list(need), way)
        if best is None or res[2] < best[2]: best = res
        w2 = [0.0] * n; nx = {}
        for i in reversed(res[0]):
            q = ops[i][0]
            w2[i] = ops[i][2] + max([w2[j] + d for j, d in succ[i]] + [0.0])
            if q in nx and q != "S": w2[i] = max(w2[i], w2[nx[q]] + ops[i][2] * QW)
            nx[q] = i
        way = [(1 - MIX) * a + MIX * b for a, b in zip(way, w2)]
    return best


def place(ops, succ, need, way):
    n = len(ops)
    ready = [0.0] * n; free = {}; cand = {}
    for i in range(n):
        if need[i] == 0: cand.setdefault(ops[i][0], []).append(i)
    seq = []; end = 0.0; bank = {}; extra = [[] for _ in range(n)]; fins = [0.0] * n

    def when(i):
        t = ready[i]
        for b in ops[i][7]:
            for qq, j in bank.get(b, {}).items():
                if qq != ops[i][0]: t = max(t, fins[j] + HOP)
        return t
    while len(seq) < n:
        best = None
        for q, l in cand.items():
            if not l: continue
            t0 = max(free.get(q, 0.0), min(when(i) for i in l))
            if best is None or t0 < best[0]: best = (t0, q)
        t0, q = best
        i = max((i for i in cand[q] if when(i) <= t0 + LOOK), key=lambda i: (way[i], -i))
        cand[q].remove(i); st = max(t0, when(i)); fin = fins[i] = st + ops[i][2]
        for b in ops[i][7]:
            extra[i] += [j for qq, j in bank.get(b, {}).items() if qq != q]
            bank.setdefault(b, {})[q] = i
        free[q] = st + 0.1 if q == "S" else fin
        seq.append(i); end = max(end, fin)
        for j, d in succ[i]:
            ready[j] = max(ready[j], fin + d); need[j] -= 1
            if need[j] == 0: cand.setdefault(ops[j][0], []).append(j)
    return seq, extra, end, fins


def replay(seq, extra, ops, dur, hop, net):
    fin = [0.0] * len(ops); free = {}
    for i in seq:
        o = ops[i]; q = o[0]; t = free.get(q, 0.0)
        for j in o[3]:
            x = fin[j] + (0.0 if q == "P" and ops[j][0] == "P" else hop)
            if x > t: t = x
        for j in extra[i]:
            if fin[j] + hop > t: t = fin[j] + hop
        for j in o[6]:
            if fin[j] + net > t: t = fin[j] + net
        fin[i] = t + dur[i]; free[q] = t + 0.1 if q == "S" else fin[i]
    return max(fin)


def tuned(ops):
    cases = [([o[2] * {"V": fv, "A": fa, "P": fp, "G": fv}.get(o[0], 1.0) + {"V": dv, "A": da}.get(o[0], 0.0) for o in ops], hop, net)
             for fv, fa, fp, hop, net, dv, da in ((1, 1, 1, 0.1, 3.0, 0, 0), (1.4, 1.35, 1.3, 0.15, 4.0, 0, 0), (1, 1, 1, 0.06, 2.0, -0.03, 0.05),
                                                  (1.15, 1.2, 1.3, 0.2, 3.0, -0.03, -0.04), (1, 1, 0.9, 0.06, 4.5, 0.02, 0))]
    cnt = {}
    for o in ops: cnt[o[8]] = cnt.get(o[8], 0) + 1
    names = sorted(k for k, v in cnt.items() if k and v >= 4)
    rnd = np.random.default_rng(SEED)
    best = None
    for it in range(TRIES + 1):
        old = dict(BIAS)
        for _ in range(int(rnd.choice((1, 2, 4))) if it else 0):
            nm = names[int(rnd.integers(len(names)))]
            BIAS[nm] = BIAS.get(nm, 0.0) + float(rnd.choice((-4, -2, -1, -0.5, 0.5, 1, 2, 4)))
        res = order(ops)
        v = [replay(res[0], res[1], ops, *cs) for cs in cases]
        sc = sum(math.log(x) for x in v)
        if best is None or sc <= best[0]: best = (sc, res, v)
        else:
            BIAS.clear(); BIAS.update(old)
    return best


PLAN = {}


def rank_program(g, core, T, topo):
    rank = T.rank_of(core)
    if rank is None:
        return
    ops = build(g, T, topo, core, rank)
    if "seq" not in PLAN:
        PLAN["seq"], PLAN["extra"], PLAN["end"], PLAN["fins"] = tuned(ops)[1]
    Qs = {"V": g.vector, "A": g.scalar, "P": g.tensor, "G": g, "S": g.sync}
    count = {}; done = {}; seen = {q: {} for q in Qs}

    def wait(q, sem, val):
        if seen[q].get(sem, 0) < val:
            Qs[q].wait_ge(T.sem[sem], val); seen[q][sem] = val

    for i in PLAN["seq"]:
        q, calls, _, deps, sem, ext = ops[i][:6]
        want = {}
        for j in list(deps) + PLAN["extra"][i]:
            if q == "P" and ops[j][0] == "P": continue
            s, v = done[j]; want[s] = max(want.get(s, 0), v)
        for s, v in ext: want[s] = v
        for s, v in want.items(): wait(q, s, v)
        for fn in calls:
            ins = fn()
            if sem is None:
                s = "e" + q; ins.then_inc(T.sem[s], 1); count[s] = count.get(s, 0) + 1
            elif sem[1] > 0:
                s = sem[0]; ins.then_inc(T.sem[s], sem[1]); count[s] = count.get(s, 0) + sem[1]
            else:
                s = sem[0]; count[s] = count.get(s, 0) - sem[1]
        done[i] = (s, count[s])
    for s, v in count.items():
        wait("G" if s == "sent" else "S", s, v)
